import numpy as np, ml_dtypes
CORES = [23,119,17,113]
N = 4
BF = ml_dtypes.bfloat16
def f(rng, *shape):
    return (rng.standard_normal(shape, dtype=np.float32) * np.exp2(rng.integers(-2, 3, shape[:-1] + (1,)))).astype(BF)
def wide(rng, *shape):
    v = f(rng, *shape).astype(np.float32); k = shape[:-2] + (1, shape[-1])
    return (v * np.exp2(rng.integers(-6, 7, k)) * (rng.random(k) > 0.0625)).astype(BF)
def gentries(a):
    return np.ascontiguousarray(a.reshape(8, 16, -1).transpose(0, 2, 1)).reshape(8, -1)
def gtable(e):
    e = np.asarray(e); return np.ascontiguousarray(e.reshape(8, -1, 16).transpose(0, 2, 1)).reshape(128, -1).astype(np.int32)
P, E, S, W, TT, CAPP = 4, 512, 4096, 128, 2048, 160
I, LS = N * S, 12
def events(x):
    return np.stack([gentries(u) for u in x]).reshape(N, 8, P, E).transpose(0, 2, 1, 3).astype(np.int64)
def unevents(e):
    return np.stack([gtable(u) for u in e.transpose(0, 2, 1, 3).reshape(N, 8, P * E)])
def shifts(sh, t):
    return np.take_along_axis(sh.astype(np.int64).reshape(N, 8, P, TT).transpose(0, 2, 1, 3), t, -1)
def evenly(rng):
    c = rng.multinomial(E, np.full(N, 2.0 ** -2), (P, 8, N)); x = np.sum(np.maximum(c - CAPP, 0), -1); c = np.minimum(c, CAPP)
    while x.any():
        i = np.argmin(c, -1)[..., None]; np.put_along_axis(c, i, np.take_along_axis(c, i, -1) + (x > 0)[..., None], -1); x = x - (x > 0)
    return c
def fully(rng):
    a = np.array(([CAPP] * (E // CAPP) + [E % CAPP] + [0] * N)[:N]); o = np.argsort(rng.random((P, 8, N, N)), -1)
    o[1::2] = o[1::2, :, :1].copy()
    return a[o]
def draw(rng, cnt, t, sh, v, crowd=False):
    pl = np.zeros((N, P, 8, E), np.int64)
    for k in range(P):
        for g in range(8):
            got = [[] for r in range(N)]
            for q in range(N):
                m = int(np.sum(cnt[k, g, :, q])); h = m // 2
                s = rng.permutation(np.append(np.arange(m - h), np.arange(S - h, S))) if crowd else rng.permutation(S)[:m]
                for r, u in enumerate(np.split(s, np.add.accumulate(cnt[k, g, :, q])[:-1])): got[r].append(u + S * q)
            for r in range(N): pl[r, k, g] = rng.permutation(np.concatenate(got[r]))
    v = v.astype(np.float32) * (1 + rng.random((N, 128, S), dtype=np.float32))
    rate = ((1 + rng.random((N, 128, 1))) * np.exp2(-rng.integers(7, 14, (N, 128, 1)))).astype(np.float32)
    return {"v": v, "last": rng.integers(-4096, 1, (N, 8, S)).astype(np.int32), "rate": rate, "sh": sh.astype(np.int32),
            "pix": unevents((pl - shifts(sh, t)) & (I - 1)), "tm": unevents(t), "pol": unevents(2 * rng.integers(0, 2, (N, P, 8, E)) - 1)}
def setup_inputs(rng):
    return draw(rng, evenly(rng), rng.integers(0, TT, (N, P, 8, E)), rng.integers(0, I, (N, 8, P * TT)), f(rng, N, 128, S))
def setup_inputs_full(rng):
    return draw(rng, fully(rng), rng.integers(0, TT, (N, P, 8, E)), rng.integers(0, I, (N, 8, P * TT)), f(rng, N, 128, S))
def setup_inputs_ends(rng):
    t = np.array([0, 1, TT - 1])[rng.integers(0, 3, (N, P, 8, E))]
    d = draw(rng, evenly(rng), t, rng.integers(0, I, (N, 8, P * TT)), f(rng, N, 128, S), True)
    d["last"] = (-4096 * rng.integers(0, 2, (N, 8, S))).astype(np.int32); return d
def setup_inputs_still(rng):
    t = np.repeat(rng.integers(0, TT, (N, P, 8, 1)), E, -1); sh = rng.integers(0, I, (N, 8, P * TT)); sh[rng.permutation(N)[:2]] = 0
    return draw(rng, evenly(rng), t, sh, f(rng, N, 128, S))
def setup_inputs_spread(rng):
    return draw(rng, evenly(rng), rng.integers(0, TT, (N, P, 8, E)), rng.integers(0, I, (N, 8, P * TT)), wide(rng, N, 128, S))
def check_inputs(d):
    bad = [] if np.isfinite(d["v"]).all() else ["v finite"]
    for a, lo, hi in (("rate", 2.0 ** -14, 2.0 ** -6), ("last", -4096, 0), ("sh", 0, I - 1), ("pix", 0, I - 1), ("tm", 0, TT - 1)):
        if not ((d[a] >= lo) & (d[a] <= hi)).all(): bad.append(a + " range")
    if not ((d["pol"] == 1) | (d["pol"] == -1)).all(): bad.append("pol is 1 or -1")
    if bad: return bad
    pl = (events(d["pix"]) + shifts(d["sh"], events(d["tm"]))) & (I - 1)
    r, k, g = np.arange(N)[:, None, None, None], np.arange(P)[None, :, None, None], np.arange(8)[None, None, :, None]
    if np.bincount(((((r * P + k) * 8 + g) * N) + (pl >> LS)).reshape(-1)).max() > CAPP: bad.append("CAPP")
    if np.unique((k * 8 + g) * I + pl).size != pl.size: bad.append("places of a packet differ")
    return bad
def reference(v, last, rate, sh, pix, tm, pol):
    V = v.astype(np.float64).reshape(N, 8, 16, S); L = last.astype(np.int64); a = rate.astype(np.float64).reshape(N, 8, 16)
    t, w = events(tm), events(pol); pl = (events(pix) + shifts(sh, t)) & (I - 1)
    y = np.zeros((N, 8, 16, P, E), np.float64); g = np.arange(8)[None, :, None]
    for k in range(P):
        q, c, now = pl[:, k] >> LS, pl[:, k] & (S - 1), TT * k + t[:, k]
        V[q, g, :, c] = V[q, g, :, c] * np.exp(-a[q, g] * (now - L[q, g, c])[..., None]) + w[:, k][..., None]
        L[q, g, c] = now
        s = np.zeros((N, 8, E, 16))
        for e in (-1, 1, -W, W): s = s + V[q, g, :, np.minimum(np.maximum(c + e, 0), S - 1)]
        y[:, :, :, k] = s.transpose(0, 1, 3, 2)
    return {"y": y.reshape(N, 128, P * E).astype(np.float32)}

@@ -1,0 +1,431 @@
+from concourse.bass import DstId, RemoteDMATransfer
+from concourse.mybir import AluOpType as A
+from concourse.mybir import ActivationFunctionType as F
+
+P, E, S, TT, CAP = 4, 512, 4096, 2048, 160
+NL = 4 * CAP
+WN = NL + S
+BIG = 1025.0
+
+
+def _sb(cols, dt="float32"):
+    return ("sbuf", [128] + (list(cols) if isinstance(cols, (list, tuple)) else [cols]), dt)
+
+
+SCRATCH = {
+    "tmI": _sb(128, "int32"), "pixI": _sb(128, "int32"), "polI": _sb(128, "int32"), "shw": _sb(512, "int32"),
+    "ratec": _sb(4), "ttab": _sb(TT), "pI": _sb(4, "int32"), "oI": _sb(4, "int32"), "pf": _sb(4), "of": _sb(4),
+    "gf": _sb(4), "iotaE": _sb(32), "Etab": _sb(32), "blk": _sb(128), "Bm": _sb(144), "omask": _sb(16),
+    "ONE": _sb(128, "bfloat16"), "M2": _sb(128, "bfloat16"), "k1": _sb(128), "k2": _sb(128), "k3": _sb(128),
+    "d0": _sb(512), "wtab": _sb(8),
+    "hI": _sb(128, "int32"), "loI": _sb(128, "int32"), "h16": _sb(128, "uint16"), "lo16": _sb(128, "uint16"),
+    "msk": _sb(P * E), "G": _sb(P * E), "X": _sb(P * E), "win": _sb(P * NL),
+    "pa": _sb(128), "pb": _sb(128), "pre": _sb(128), "pixr": _sb(128),
+    "uI": _sb(128, "int32"), "qI": _sb(128, "int32"), "cI": _sb(128, "int32"), "cod": _sb(128),
+    "ind": _sb(512, "bfloat16"), "scn": _sb(512), "pos": _sb(512), "m1": _sb(256), "m2": _sb(128),
+    "slot": _sb(128, "uint16"),
+    "ev0": _sb(32), "ev1": _sb([3, 30]), "land0": _sb([4, 12]), "land1": _sb([4, 32]),
+    "x0": _sb(40, "int32"), "c0": _sb(40, "int32"), "t0": _sb(40, "int32"),
+    "x1": _sb([4, 30], "int32"), "c1": _sb([4, 30], "int32"), "t1": _sb([4, 30], "int32"),
+    "cs16": _sb(160, "uint16"), "t16": _sb(160, "uint16"), "p16": _sb(160, "uint16"),
+    "nb0": _sb([4, 40], "uint16"), "nb1": _sb([12, 40], "uint16"),
+    "V": _sb(WN), "L": _sb(WN, "int32"),
+    "At": _sb(P * NL), "Wt": _sb(P * NL), "dt": _sb(P * NL), "Ex": _sb(P * NL), "tmp": _sb(P * NL),
+    "ag": _sb(P * 3 * NL), "ans0": _sb(1120), "ans1": _sb(1120), "ans2": _sb(1120), "ans3": _sb(1120),
+    "yst": _sb(P * E),
+    "PS": ("psum", [128, 512], "float32"), "PC": ("psum", [128, 512], "float32"), "PM": ("psum", [128, 512], "float32"),
+    "PW0": ("psum", [128, 512], "float32"), "PW1": ("psum", [128, 512], "float32"),
+    "PW2": ("psum", [128, 512], "float32"), "PW3": ("psum", [128, 512], "float32"),
+}
+SEMAPHORES = ["cv", "cs", "ct", "cg", "ltm", "lsh", "lpp", "lL", "lv", "lrate", "evA", "evB", "an0", "an1", "an2", "an3",
+              "sent", "accA", "accB0", "accB1", "st"]
+
+
+def _bits(es):
+    m = 0
+    for e in es:
+        m |= 1 << e
+    return m
+
+
+def _share(topo, src, dsts, near_most):
+    far = [d for d in dsts if topo.chip(d) != topo.chip(src)]
+    near = [d for d in dsts if topo.chip(d) == topo.chip(src)]
+    out, used = {}, []
+    for grp, most in ((far, 16), (near, near_most)):
+        for i, d in enumerate(grp):
+            free = [e for e in topo.engines(src, d) if e not in used]
+            n = min(len(free) // (len(grp) - i), most)
+            while n & (n - 1):
+                n -= 1
+            out[d] = free[:n]
+            used += free[:n]
+    return out
+
+
+def rank_program(g, core, T, topo):
+    r = T.rank_of(core)
+    if r is None:
+        return
+    cores = list(T.cores)
+    N = len(cores)
+    Q = {"v": g.vector, "s": g.scalar, "t": g.tensor, "g": g, "y": g.sync}
+    cnt = {}
+    waited = {q: {} for q in Q}
+
+    def wait(q, *toks):
+        for tk in toks:
+            if tk is None:
+                continue
+            s, n = tk
+            if waited[q].get(s, 0) < n:
+                Q[q].wait_ge(T.sem[s], n)
+                waited[q][s] = n
+
+    def fin(ins, s, n):
+        ins.then_inc(T.sem[s], n)
+        cnt[s] = cnt.get(s, 0) + n
+        return (s, cnt[s])
+
+    def ts(out, in0, s1, s2, op0, op1=None, dep=()):
+        wait("v", *dep)
+        if op1 is None:
+            return fin(g.vector.tensor_scalar(out, in0, s1, None, op0), "cv", 1)
+        return fin(g.vector.tensor_scalar(out, in0, s1, s2, op0, op1), "cv", 1)
+
+    def tt(out, in0, in1, op, dep=()):
+        wait("v", *dep)
+        return fin(g.vector.tensor_tensor(out, in0, in1, op), "cv", 1)
+
+    def cp(out, in_, dep=()):
+        wait("v", *dep)
+        return fin(g.vector.tensor_copy(out, in_), "cv", 1)
+
+    def ms(ap, c, dep=()):
+        wait("v", *dep)
+        return fin(g.vector.memset(ap, c), "cv", 1)
+
+    def act(out, in_, func=F.Identity, dep=(), **kw):
+        wait("s", *dep)
+        return fin(g.scalar.activation(out, in_, func, **kw), "cs", 1)
+
+    def iota(out, pat, base, cm, flag=True):
+        if flag:
+            return fin(g.iota(out, pat, base, cm, allow_small_or_imprecise_dtypes=True), "cg", 1)
+        return fin(g.iota(out, pat, base, cm), "cg", 1)
+
+    def dma(q, out, in_, s, dep=(), **kw):
+        wait(q, *dep)
+        return fin(Q[q].dma_start(out, in_, **kw), s, 16)
+
+    def to_lists(out, buf, c0, n, dep):
+        wait("t", *dep)
+        for o in range(16):
+            ins = g.tensor.matmul(out, T.Bm[:, 15 - o:143 - o], buf[:, c0 + o:c0 + n:16], o == 0, o == 15)
+        return fin(ins, "ct", 1)
+
+    def remote(items, sem, dep):
+        wait("g", *dep)
+        trs, tot = [], 0
+        for d, es, srcs, dst in items:
+            rid, pid, _ = topo.addr(d)
+            trs.append(RemoteDMATransfer(dst_ids=[DstId(rid=rid, pnc=pid)], dma_engine_mask=_bits(es),
+                                         remote_sem=T.sem[sem], srcs=srcs, dsts=[dst], alu_op=1 if len(srcs) > 1 else 0))
+            tot += len(es)
+        g.remote_dma_fused(trs, local_sem=T.sem.sent)
+        cnt["sent"] = cnt.get("sent", 0) + tot
+
+    def ev_dst(a):
+        return [cores[(a + 3 - j) % N] for j in range(3)]
+
+    def an_dst(a):
+        return [cores[(a - 3 + j) % N] for j in range(3)]
+
+    def ev_eng(a):
+        return _share(topo, cores[a], ev_dst(a), 4)
+
+    def an_eng(a):
+        return _share(topo, cores[a], an_dst(a), 16)
+
+    def tail_plan(a):
+        ds = an_dst(a)
+        far = [j for j in range(3) if topo.chip(ds[j]) != topo.chip(cores[a])]
+        near = [j for j in range(3) if j not in far]
+        first, second = far[:1] + near, far[1:]
+        eng = dict(_share(topo, cores[a], [ds[j] for j in first], 16))
+        eng.update(_share(topo, cores[a], [ds[j] for j in second], 16))
+        return far, near, first, second, eng
+
+    others = [a for a in range(N) if a != r]
+    n_ev = sum(len(ev_eng(a)[core]) for a in others)
+    n_an = sum(len(an_eng(a)[core]) for a in others)
+    n_tail = sum(len(tail_plan(a)[4][core]) for a in others)
+
+    l_tm = dma("y", T.tmI[:], T.tm[:], "ltm")
+    l_sh = dma("s", T.shw[:], T.sh[:], "lsh")
+    dma("y", T.pixI[:], T.pix[:], "lpp")
+    l_pp = dma("y", T.polI[:], T.pol[:], "lpp")
+    wait("y", l_tm, l_sh, l_pp)
+    for o in range(16):
+        l_L = dma("y", T.L[o::16, NL:WN], T.last[:], "lL")
+    l_v = dma("y", T.V[:, NL:WN], T.v[:], "lv")
+
+    i_p = iota(T.pI[:, 0:1], [[0, 1]], 0, 1, False)
+    i_e = iota(T.iotaE[:], [[4, 4], [1, 8]], 0, 0)
+    i_t0 = iota(T.ttab[:, 0:NL], [[1, NL]], 0, 0)
+    i_b = iota(T.blk[:], [[16, 8], [0, 16]], 0, 0)
+    l_rate = dma("g", T.ratec[:, 0:1], T.rate[:], "lrate", allow_slow_non_contiguous=True)
+    i_t1 = iota(T.ttab[:, NL:TT], [[1, TT - NL]], NL, 0)
+
+    z_d = ms(T.d0[:], 1.0e4)
+    z_w = ms(T.wtab[:], 1.0)
+    z_V = ms(T.V[:, 0:NL], 0.0)
+    c_o = ts(T.oI[:, 0:1], T.pI[:, 0:1], 15, None, A.bitwise_and, dep=[i_p])
+    c_p = cp(T.pf[:, 0:1], T.pI[:, 0:1])
+    z_L = ms(T.L[:, 0:NL], 0)
+    c_of = cp(T.of[:, 0:1], T.oI[:, 0:1], dep=[c_o])
+    z_w = ms(T.wtab[:, 1:2], -1.0, dep=[z_w])
+    c_E = ts(T.Etab[:], T.iotaE[:], T.of[:, 0:1], None, A.is_equal, dep=[c_of, i_e])
+    c_g = tt(T.gf[:, 0:1], T.pf[:, 0:1], T.of[:, 0:1], A.subtract, dep=[c_p])
+
+    z_win = [None] * P
+    for k in (0, 1):
+        z_win[k] = act(T.win[:, NL * k:NL * (k + 1)], T.ttab[:, 0:NL], scale=1.0 / 16, dep=[i_t0])
+
+    a = ts(T.hI[:], T.tmI[:], 9, None, A.arith_shift_right, dep=[l_tm])
+    b = ts(T.loI[:], T.tmI[:], 511, None, A.bitwise_and)
+    s_h = cp(T.h16[:], T.hI[:], dep=[a])
+    s_lo = cp(T.lo16[:], T.loI[:], dep=[b])
+    c_B = ts(T.Bm[:], T.ttab[:, 0:144], -15.0, T.gf[:, 0:1], A.add, A.is_equal, dep=[c_g, i_t0])
+    c_om = ts(T.omask[:], T.ttab[:, 0:16], T.of[:, 0:1], None, A.is_equal)
+    s_m = [act(T.msk[:, E * k:E * (k + 1)], T.Etab[:, 8 * k:8 * k + 8].indirect(T.h16[:, 32 * k:32 * k + 32]),
+               dep=[s_h, c_E]) for k in range(P)]
+    for k in (2, 3):
+        z_win[k] = act(T.win[:, NL * k:NL * (k + 1)], T.ttab[:, 0:NL], scale=1.0 / 16)
+    s_pe = None
+    for k in range(P):
+        s_g = tt(T.G[:, E * k:E * (k + 1)], T.shw[:, 0:512].indirect(T.lo16[:, 32 * k:32 * k + 32]),
+                 T.msk[:, E * k:E * (k + 1)], A.mult, dep=[s_lo, l_sh, s_m[k]])
+        if k & 1:
+            h = k >> 1
+            s_pe = to_lists(T.PS[:, 64 * h:64 * h + 64], T.G, 1024 * h, 1024, [s_g, c_B])
+
+    c_1 = ts(T.ONE[:], T.blk[:], T.gf[:, 0:1], None, A.is_equal, dep=[i_b])
+    a = ts(T.k1[:], T.ttab[:, 0:128], T.pf[:, 0:1], -1.0, A.is_lt, A.mult)
+    b = ts(T.k3[:], T.ttab[:, 0:128], T.pf[:, 0:1], BIG - 1.0, A.is_equal, A.mult)
+    e_r = ts(T.pixr[:], T.pixI[:], float(S * ((N - r) % N)), None, A.add, dep=[l_pp])
+    a = tt(T.k2[:], T.k1[:], T.ONE[:], A.mult, dep=[a, c_1])
+    e_a = ts(T.pa[:], T.tmI[:], 8192.0, float(NL - 2 ** 23), A.mult, A.add)
+    e_b = ts(T.pb[:], T.polI[:], float(2 ** 23), None, A.mult)
+    c_2 = tt(T.M2[:], T.k2[:], T.k3[:], A.add, dep=[a, b])
+    for i in range(4):
+        z_d2 = ms(T.d0[:, 128 * i:128 * (i + 1):32], float(CAP * (3 - i)), dep=[z_d])
+    e_p = tt(T.pre[:], T.pa[:], T.pb[:], A.add, dep=[e_a, e_b])
+
+    u = tt(T.uI[:], T.PS[:, 0:128], T.pixr[:], A.add, dep=[s_pe, e_r])
+    q = ts(T.qI[:], T.uI[:], 12, 3, A.arith_shift_right, A.bitwise_and, dep=[u])
+    c = ts(T.cI[:], T.uI[:], S - 1, None, A.bitwise_and)
+    for i in range(4):
+        n_i = ts(T.ind[:, 128 * i:128 * (i + 1)], T.qI[:], float(i), None, A.is_equal, dep=[q])
+    wait("t", n_i, c_1, c_2)
+    n_c = fin(g.tensor.matmul(T.PC[:], T.ONE[:], T.ind[:], True, True), "ct", 1)
+    n_m = fin(g.tensor.matmul(T.PM[:], T.M2[:], T.ind[:], True, True), "ct", 1)
+    cod = tt(T.cod[:], T.cI[:], T.pre[:], A.add, dep=[c, e_p])
+    for o in range(16):
+        x_all = act(T.X[:, o::16], T.cod[:], scale=T.omask[:, o:o + 1], dep=[cod, c_om])
+    wait("v", n_c, z_d2)
+    a = fin(g.vector.tensor_tensor_scan(T.scn[:], T.d0[:], T.PC[:], 1.0e4, A.min, A.add), "cv", 1)
+    a = tt(T.pos[:], T.scn[:], T.PM[:], A.add, dep=[a, n_m])
+    a = tt(T.m1[:], T.pos[:, 0:256], T.pos[:, 256:512], A.max, dep=[a])
+    a = tt(T.m2[:], T.m1[:, 0:128], T.m1[:, 128:256], A.max, dep=[a])
+    slot = ts(T.slot[:], T.m2[:], -BIG, None, A.add, dep=[a])
+
+    PW = [T.PW0, T.PW1, T.PW2, T.PW3]
+    w_pe = []
+    for k in range(P):
+        a = cp(T.win[:, NL * k:NL * (k + 1)].indirect(T.slot[:, 32 * k:32 * k + 32]), T.X[:, E * k:E * (k + 1)],
+               dep=[slot, x_all, z_win[k]])
+        w_pe.append(to_lists(PW[k][:, 0:40], T.win, NL * k, NL, [a]))
+
+    def out_lists(k):
+        if k == 0:
+            a = act(T.ev0[:, 0:30], PW[0][:, 0:30], dep=[w_pe[0]])
+            return a, act(T.land0[:, 3, 0:10], PW[0][:, 30:40])
+        a = act(T.ev1[:, :, 10 * k - 10:10 * k], PW[k][:, 0:30], dep=[w_pe[k]])
+        return a, act(T.land1[:, 3, 10 * k - 10:10 * k], PW[k][:, 30:40])
+
+    ed, ee = ev_dst(r), ev_eng(r)
+    a, own0 = out_lists(0)
+    remote([(ed[j], ee[ed[j]], [T.ev0[:, 10 * j:10 * j + 10]], T.land0[:, j, 0:10]) for j in range(3)], "evA", [a])
+    out_lists(1)
+    out_lists(2)
+
+    def nbrs(out, cin, dep):
+        for n, (d, lim, op) in enumerate(((-1.0, NL, A.max), (1.0, WN - 1, A.min), (-128.0, NL, A.max),
+                                          (128.0, WN - 1, A.min))):
+            tk = ts(out[:, :, 10 * n:10 * n + 10], cin, d, float(lim), A.add, op, dep=dep)
+        return tk
+
+    def col(buf, k):
+        return buf[:, 40 * k:40 * k + 40]
+
+    def row(buf, k):
+        return buf[:, NL * k:NL * (k + 1)]
+
+    def nb(k, j, n=None):
+        buf, i = (T.nb0, j) if k == 0 else (T.nb1, 3 * j + k - 1)
+        return buf[:, i, :] if n is None else buf[:, i, 10 * n:10 * n + 10]
+
+    d_t, d_c, d_p, d_n = [None] * P, [None] * P, [None] * P, [None] * P
+    x = cp(T.x0[:], T.land0[:, :, 0:10], dep=[("evA", n_ev), own0])
+    a = ts(T.t0[:], T.x0[:], 13, TT - 1, A.arith_shift_right, A.bitwise_and, dep=[x])
+    b = ts(T.c0[:], T.x0[:], 8191, None, A.bitwise_and)
+    d_t[0] = cp(col(T.t16, 0), T.t0[:], dep=[a])
+    d_p[0] = ts(col(T.p16, 0), T.x0[:], 0.0, None, A.is_lt)
+    d_c[0] = cp(col(T.cs16, 0), T.c0[:], dep=[b])
+    d_n[0] = nbrs(T.nb0, T.c0[:], [b])
+
+    tA, tW, tL, tE, tV, tS = ([None] * P for _ in range(6))
+
+    def times(k):
+        tA[k] = act(row(T.At, k), T.ttab[:, 0:TT].indirect(col(T.t16, k)), bias=float(TT * k), dep=[d_t[k], i_t1])
+
+    def pols(k):
+        tW[k] = act(row(T.Wt, k), T.wtab[:, 0:8].indirect(col(T.p16, k)), dep=[d_p[k], z_w])
+
+    last_sL = [None]
+
+    def get_last(k):
+        tL[k] = tt(row(T.dt, k), T.L[:, 0:WN].indirect(col(T.cs16, k)), row(T.At, k), A.subtract,
+                   dep=[d_c[k], tA[k], l_L, z_L, last_sL[0]])
+
+    def put_last(k):
+        last_sL[0] = cp(T.L[:, 0:WN].indirect(col(T.cs16, k)), row(T.At, k), dep=[tL[k]])
+
+    def decay(k):
+        tE[k] = act(row(T.Ex, k), row(T.dt, k), F.Exp, scale=T.ratec[:, 0:1], dep=[tL[k], l_rate])
+
+    def get_state(k):
+        tV[k] = tt(row(T.tmp, k), T.V[:, 0:WN].indirect(col(T.cs16, k)), row(T.Ex, k), A.mult,
+                   dep=[tE[k], l_v, z_V, tS[k - 1] if k else None])
+
+    def put_state(k, readers):
+        tS[k] = tt(T.V[:, 0:WN].indirect(col(T.cs16, k)), row(T.tmp, k), row(T.Wt, k), A.add,
+                   dep=[tV[k], tW[k]] + readers)
+
+    ANS = [T.ans0, T.ans1, T.ans2, T.ans3]
+
+    def ag(k, j, n=None):
+        c0 = NL * (3 * k + j)
+        return T.ag[:, c0:c0 + NL] if n is None else T.ag[:, c0 + CAP * n:c0 + CAP * (n + 1)]
+
+    def four(k, j):
+        out = ANS[k][:, 3 * CAP:3 * CAP + NL] if j == 3 else ag(k, j)
+        return act(out, T.V[:, 0:WN].indirect(nb(k, j)), dep=[tS[k], d_n[k]])
+
+    def summed(k, j):
+        out = ANS[k][:, 3 * CAP:NL] if j == 3 else ag(k, j, 0)
+        tk = cp(out, T.V[:, 0:WN].indirect(nb(k, j, 0)), dep=[tS[k], d_n[k]])
+        for n in range(1, 4):
+            tk = tt(out, T.V[:, 0:WN].indirect(nb(k, j, n)), out, A.add, dep=[tk])
+        return tk
+
+    ad, ae = an_dst(r), an_eng(r)
+
+    def send(k, dep):
+        remote([(ad[j], ae[ad[j]], [ag(k, j, n) for n in range(4)], ANS[k][:, CAP * j:CAP * (j + 1)]) for j in range(3)],
+               "an%d" % k, dep)
+
+    def own_sum(k, dep):
+        a = dma("g", ANS[k][:, 480:800], ANS[k][:, 800:1120], "accA", dep=dep, accum_op=A.add)
+        return dma("g", ANS[k][:, 480:640], ANS[k][:, 640:800], "accB%d" % k, dep=[a], accum_op=A.add)
+
+    def pick(q, k, c0, c1, dep):
+        out = T.yst[:, E * k + 16 * c0:E * k + 16 * c1]
+        src = ANS[k][:, 0:NL].indirect(T.slot[:, 32 * k + c0:32 * k + c1])
+        return cp(out, src, dep=dep) if q == "v" else act(out, src, dep=dep)
+
+    def store(k, dep):
+        return dma("y", T.y[:, E * k:E * (k + 1)], T.yst[:, E * k:E * (k + 1)], "st", dep=dep)
+
+    times(0)
+    a, own1 = out_lists(3)
+    remote([(ed[j], ee[ed[j]], [T.ev1[:, j, :]], T.land1[:, j, 0:30]) for j in range(3)], "evB", [a])
+    pols(0)
+    get_last(0)
+    decay(0)
+    put_last(0)
+    get_state(0)
+
+    x = cp(T.x1[:], T.land1[:, :, 0:30], dep=[("evB", n_ev), own1])
+    a1 = ts(T.t1[:], T.x1[:], 13, TT - 1, A.arith_shift_right, A.bitwise_and, dep=[x])
+    b1 = ts(T.c1[:], T.x1[:], 8191, None, A.bitwise_and)
+
+    def lists(k):
+        cs = slice(10 * k - 10, 10 * k)
+        d_t[k] = cp(col(T.t16, k), T.t1[:, :, cs], dep=[a1])
+        d_p[k] = ts(col(T.p16, k), T.x1[:, :, cs], 0.0, None, A.is_lt)
+        d_c[k] = cp(col(T.cs16, k), T.c1[:, :, cs], dep=[b1])
+
+    lists(1)
+    put_state(0, [])
+    times(1)
+    pols(1)
+    own = [None] * P
+    for k in (0, 1):
+        get_last(k + 1)
+        four(k, 0)
+        decay(k + 1)
+        if k == 0:
+            lists(2)
+            lists(3)
+            d_n[1] = d_n[2] = d_n[3] = nbrs(T.nb1, T.c1[:], [b1])
+        put_last(k + 1)
+        get_state(k + 1)
+        four(k, 1)
+        a = four(k, 2)
+        send(k, [a])
+        a = four(k, 3)
+        own[k] = own_sum(k, [a])
+        put_state(k + 1, [a])
+        times(k + 2)
+        pols(k + 2)
+    get_last(3)
+    four(2, 0)
+    decay(3)
+    own[2] = summed(2, 3)
+    get_state(3)
+    four(2, 1)
+    a = four(2, 2)
+    send(2, [a])
+    y0 = pick("v", 0, 0, 32, [("an0", n_an), own[0]])
+    store(0, [y0])
+    put_state(3, [a])
+    y1 = pick("s", 1, 0, 32, [("an1", n_an), own[1]])
+    store(1, [y1])
+
+    far, near, first, second, te = tail_plan(r)
+    done = {}
+    for j in far:
+        done[j] = summed(3, j)
+    for j in near:
+        done[j] = four(3, j)
+    a = four(3, 3)
+
+    def tail(js):
+        remote([(ad[j], te[ad[j]], [ag(3, j, 0)] if j in far else [ag(3, j, n) for n in range(4)],
+                 ANS[3][:, CAP * j:CAP * (j + 1)]) for j in js], "an3", [done[j] for j in js])
+
+    tail(first)
+    tail(second)
+    a = tt(ANS[3][:, 480:800], ANS[3][:, 480:800], ANS[3][:, 800:1120], A.add, dep=[a])
+    own[3] = tt(ANS[3][:, 480:640], ANS[3][:, 480:640], ANS[3][:, 640:800], A.add, dep=[a])
+    y2 = pick("s", 2, 0, 32, [("an2", n_an), own[2]])
+    store(2, [y2])
+    ya = pick("v", 3, 0, 16, [("an3", n_tail), own[3]])
+    yb = pick("s", 3, 16, 32, [("an3", n_tail), own[3]])
+    a = store(3, [ya, yb])
+    wait("y", a)
+    for s, n in cnt.items():
+        if max(waited[q].get(s, 0) for q in Q) < n:
+            wait("g", (s, n))

@@ -6,6 +6,7 @@ P, E, S, TT, CAP = 4, 512, 4096, 2048, 160
 NL = 4 * CAP
 WN = NL + S
 BIG = 1025.0
+BATCH = [[0], [1], [2, 3]]
 
 
 def _sb(cols, dt="float32"):
@@ -15,30 +16,33 @@ def _sb(cols, dt="float32"):
 SCRATCH = {
     "tmI": _sb(128, "int32"), "pixI": _sb(128, "int32"), "polI": _sb(128, "int32"), "shw": _sb(512, "int32"),
     "ratec": _sb(4), "ttab": _sb(TT), "pI": _sb(4, "int32"), "oI": _sb(4, "int32"), "pf": _sb(4), "of": _sb(4),
-    "gf": _sb(4), "iotaE": _sb(32), "Etab": _sb(32), "blk": _sb(128), "Bm": _sb(144), "omask": _sb(16),
+    "gf": _sb(4), "iotaE": _sb(32), "Etab": _sb(32), "blk": _sb(128), "Bm": _sb(144),
+    "oiota": _sb(E), "omask": _sb(E), "rep": _sb(128, "uint16"),
     "ONE": _sb(128, "bfloat16"), "M2": _sb(128, "bfloat16"), "k1": _sb(128), "k2": _sb(128), "k3": _sb(128),
-    "d0": _sb(512), "wtab": _sb(8),
+    "d0": _sb(256), "wtab": _sb(8),
     "hI": _sb(128, "int32"), "loI": _sb(128, "int32"), "h16": _sb(128, "uint16"), "lo16": _sb(128, "uint16"),
     "msk": _sb(P * E), "G": _sb(P * E), "X": _sb(P * E), "win": _sb(P * NL),
     "pa": _sb(128), "pb": _sb(128), "pre": _sb(128), "pixr": _sb(128),
-    "uI": _sb(128, "int32"), "qI": _sb(128, "int32"), "cI": _sb(128, "int32"), "cod": _sb(128),
+    "uI": _sb(128, "int32"), "qI": _sb(128, "int32"), "cI": _sb(128, "int32"), "cod0": _sb(64), "cod1": _sb(64),
     "ind": _sb(512, "bfloat16"), "scn": _sb(512), "pos": _sb(512), "m1": _sb(256), "m2": _sb(128),
     "slot": _sb(128, "uint16"),
-    "ev0": _sb(32), "ev1": _sb([3, 30]), "land0": _sb([4, 12]), "land1": _sb([4, 32]),
-    "x0": _sb(40, "int32"), "c0": _sb(40, "int32"), "t0": _sb(40, "int32"),
-    "x1": _sb([4, 30], "int32"), "c1": _sb([4, 30], "int32"), "t1": _sb([4, 30], "int32"),
     "cs16": _sb(160, "uint16"), "t16": _sb(160, "uint16"), "p16": _sb(160, "uint16"),
-    "nb0": _sb([4, 40], "uint16"), "nb1": _sb([12, 40], "uint16"),
-    "V": _sb(WN), "L": _sb(WN, "int32"),
+    "V": _sb(WN), "L": _sb(WN, "int32"), "Ld": ("dram", [8, 4, S], "int32"),
     "At": _sb(P * NL), "Wt": _sb(P * NL), "dt": _sb(P * NL), "Ex": _sb(P * NL), "tmp": _sb(P * NL),
     "ag": _sb(P * 3 * NL), "ans0": _sb(1120), "ans1": _sb(1120), "ans2": _sb(1120), "ans3": _sb(1120),
     "yst": _sb(P * E),
-    "PS": ("psum", [128, 512], "float32"), "PC": ("psum", [128, 512], "float32"), "PM": ("psum", [128, 512], "float32"),
-    "PW0": ("psum", [128, 512], "float32"), "PW1": ("psum", [128, 512], "float32"),
-    "PW2": ("psum", [128, 512], "float32"), "PW3": ("psum", [128, 512], "float32"),
 }
-SEMAPHORES = ["cv", "cs", "ct", "cg", "ltm", "lsh", "lpp", "lL", "lv", "lrate", "evA", "evB", "an0", "an1", "an2", "an3",
-              "sent", "accA", "accB0", "accB1", "st"]
+for _b, _ks in enumerate(BATCH):
+    _n = 10 * len(_ks)
+    SCRATCH["ev%d" % _b] = _sb([3, _n])
+    SCRATCH["land%d" % _b] = _sb([4, (_n + 3) // 4 * 4])
+    for _x in "xct":
+        SCRATCH["%s%d" % (_x, _b)] = _sb([4, _n], "int32")
+    SCRATCH["nb%d" % _b] = _sb([4 * len(_ks), 40], "uint16")
+for _x in ("PS0", "PS1", "PC", "PM", "PW0", "PW1", "PW2", "PW3"):
+    SCRATCH[_x] = ("psum", [128, 512], "float32")
+SEMAPHORES = ["cv", "cs", "ct", "cg", "ltm", "lsh", "lpp", "lD", "lL", "lv", "lrate", "ev0", "ev1", "ev2",
+              "an0", "an1", "an2", "an3", "sent", "accA", "accB0", "accB1", "st"]
 
 
 def _bits(es):
@@ -147,124 +151,139 @@ def rank_program(g, core, T, topo):
     def an_eng(a):
         return _share(topo, cores[a], an_dst(a), 16)
 
-    def tail_plan(a):
-        ds = an_dst(a)
-        far = [j for j in range(3) if topo.chip(ds[j]) != topo.chip(cores[a])]
-        near = [j for j in range(3) if j not in far]
-        first, second = far[:1] + near, far[1:]
-        eng = dict(_share(topo, cores[a], [ds[j] for j in first], 16))
-        eng.update(_share(topo, cores[a], [ds[j] for j in second], 16))
-        return far, near, first, second, eng
-
     others = [a for a in range(N) if a != r]
     n_ev = sum(len(ev_eng(a)[core]) for a in others)
     n_an = sum(len(an_eng(a)[core]) for a in others)
-    n_tail = sum(len(tail_plan(a)[4][core]) for a in others)
 
     l_tm = dma("y", T.tmI[:], T.tm[:], "ltm")
     l_sh = dma("s", T.shw[:], T.sh[:], "lsh")
     dma("y", T.pixI[:], T.pix[:], "lpp")
     l_pp = dma("y", T.polI[:], T.pol[:], "lpp")
-    wait("y", l_tm, l_sh, l_pp)
-    for o in range(16):
-        l_L = dma("y", T.L[o::16, NL:WN], T.last[:], "lL")
-    l_v = dma("y", T.V[:, NL:WN], T.v[:], "lv")
+    for x in range(4):
+        l_D = dma("s" if x < 2 else "y", T.Ld[:, x, :], T.last[:], "lD")
+    for m in range(4):
+        l_L = dma("y", T.L[m::4, NL:WN], T.Ld[:], "lL", dep=[l_D])
 
     i_p = iota(T.pI[:, 0:1], [[0, 1]], 0, 1, False)
     i_e = iota(T.iotaE[:], [[4, 4], [1, 8]], 0, 0)
-    i_t0 = iota(T.ttab[:, 0:NL], [[1, NL]], 0, 0)
+    i_ta = iota(T.ttab[:, 0:144], [[1, 144]], 0, 0)
     i_b = iota(T.blk[:], [[16, 8], [0, 16]], 0, 0)
+    i_t0 = iota(T.ttab[:, 144:NL], [[1, NL - 144]], 144, 0)
+    i_o = iota(T.oiota[:], [[0, 32], [1, 16]], 0, 0)
+    i_d = iota(T.d0[:], [[-CAP, 4], [0, 2], [1000, 32]], 3 * CAP, 0)
+    l_v = dma("g", T.V[:, NL:WN], T.v[:], "lv")
     l_rate = dma("g", T.ratec[:, 0:1], T.rate[:], "lrate", allow_slow_non_contiguous=True)
     i_t1 = iota(T.ttab[:, NL:TT], [[1, TT - NL]], NL, 0)
 
-    z_d = ms(T.d0[:], 1.0e4)
     z_w = ms(T.wtab[:], 1.0)
-    z_V = ms(T.V[:, 0:NL], 0.0)
+    z_L = ms(T.L[:, 0:NL], 0)
     c_o = ts(T.oI[:, 0:1], T.pI[:, 0:1], 15, None, A.bitwise_and, dep=[i_p])
     c_p = cp(T.pf[:, 0:1], T.pI[:, 0:1])
-    z_L = ms(T.L[:, 0:NL], 0)
-    c_of = cp(T.of[:, 0:1], T.oI[:, 0:1], dep=[c_o])
     z_w = ms(T.wtab[:, 1:2], -1.0, dep=[z_w])
-    c_E = ts(T.Etab[:], T.iotaE[:], T.of[:, 0:1], None, A.is_equal, dep=[c_of, i_e])
-    c_g = tt(T.gf[:, 0:1], T.pf[:, 0:1], T.of[:, 0:1], A.subtract, dep=[c_p])
+    c_of = cp(T.of[:, 0:1], T.oI[:, 0:1], dep=[c_o])
+    a = ts(T.k1[:], T.ttab[:, 0:128], T.pf[:, 0:1], -1.0, A.is_lt, A.mult, dep=[c_p, i_ta])
+    c_g = tt(T.gf[:, 0:1], T.pf[:, 0:1], T.of[:, 0:1], A.subtract, dep=[c_of])
+    c_E = ts(T.Etab[:], T.iotaE[:], T.of[:, 0:1], None, A.is_equal, dep=[i_e])
+    b = ts(T.k3[:], T.ttab[:, 0:128], T.pf[:, 0:1], BIG - 1.0, A.is_equal, A.mult)
+    c_1 = ts(T.ONE[:], T.blk[:], T.gf[:, 0:1], None, A.is_equal, dep=[i_b, c_g])
+    c_B = ts(T.Bm[:], T.ttab[:, 0:144], -15.0, T.gf[:, 0:1], A.add, A.is_equal)
+    a = tt(T.k2[:], T.k1[:], T.ONE[:], A.mult, dep=[a, c_1])
+    c_r = cp(T.rep[:, 0:64], T.ttab[:, 0:64])
 
     z_win = [None] * P
-    for k in (0, 1):
+
+    def empty(k):
         z_win[k] = act(T.win[:, NL * k:NL * (k + 1)], T.ttab[:, 0:NL], scale=1.0 / 16, dep=[i_t0])
 
-    a = ts(T.hI[:], T.tmI[:], 9, None, A.arith_shift_right, dep=[l_tm])
-    b = ts(T.loI[:], T.tmI[:], 511, None, A.bitwise_and)
-    s_h = cp(T.h16[:], T.hI[:], dep=[a])
-    s_lo = cp(T.lo16[:], T.loI[:], dep=[b])
-    c_B = ts(T.Bm[:], T.ttab[:, 0:144], -15.0, T.gf[:, 0:1], A.add, A.is_equal, dep=[c_g, i_t0])
-    c_om = ts(T.omask[:], T.ttab[:, 0:16], T.of[:, 0:1], None, A.is_equal)
+    a1 = ts(T.hI[:], T.tmI[:], 9, None, A.arith_shift_right, dep=[l_tm])
+    b1 = ts(T.loI[:], T.tmI[:], 511, None, A.bitwise_and)
+    s_h = cp(T.h16[:], T.hI[:], dep=[a1])
+    s_lo = cp(T.lo16[:], T.loI[:], dep=[b1])
     s_m = [act(T.msk[:, E * k:E * (k + 1)], T.Etab[:, 8 * k:8 * k + 8].indirect(T.h16[:, 32 * k:32 * k + 32]),
                dep=[s_h, c_E]) for k in range(P)]
-    for k in (2, 3):
-        z_win[k] = act(T.win[:, NL * k:NL * (k + 1)], T.ttab[:, 0:NL], scale=1.0 / 16)
-    s_pe = None
-    for k in range(P):
-        s_g = tt(T.G[:, E * k:E * (k + 1)], T.shw[:, 0:512].indirect(T.lo16[:, 32 * k:32 * k + 32]),
-                 T.msk[:, E * k:E * (k + 1)], A.mult, dep=[s_lo, l_sh, s_m[k]])
-        if k & 1:
-            h = k >> 1
-            s_pe = to_lists(T.PS[:, 64 * h:64 * h + 64], T.G, 1024 * h, 1024, [s_g, c_B])
-
-    c_1 = ts(T.ONE[:], T.blk[:], T.gf[:, 0:1], None, A.is_equal, dep=[i_b])
-    a = ts(T.k1[:], T.ttab[:, 0:128], T.pf[:, 0:1], -1.0, A.is_lt, A.mult)
-    b = ts(T.k3[:], T.ttab[:, 0:128], T.pf[:, 0:1], BIG - 1.0, A.is_equal, A.mult)
-    e_r = ts(T.pixr[:], T.pixI[:], float(S * ((N - r) % N)), None, A.add, dep=[l_pp])
-    a = tt(T.k2[:], T.k1[:], T.ONE[:], A.mult, dep=[a, c_1])
-    e_a = ts(T.pa[:], T.tmI[:], 8192.0, float(NL - 2 ** 23), A.mult, A.add)
-    e_b = ts(T.pb[:], T.polI[:], float(2 ** 23), None, A.mult)
+    empty(0)
+    empty(1)
     c_2 = tt(T.M2[:], T.k2[:], T.k3[:], A.add, dep=[a, b])
-    for i in range(4):
-        z_d2 = ms(T.d0[:, 128 * i:128 * (i + 1):32], float(CAP * (3 - i)), dep=[z_d])
+    e_a = ts(T.pa[:], T.tmI[:], 8192.0, float(NL - 2 ** 23), A.mult, A.add)
+    e_b = ts(T.pb[:], T.polI[:], float(2 ** 23), None, A.mult, dep=[l_pp])
+    e_r = ts(T.pixr[:], T.pixI[:], float(S * ((N - r) % N)), None, A.add)
+    PS = [T.PS0, T.PS1]
+    s_g = []
+    for k in range(P):
+        s_g.append(tt(T.G[:, E * k:E * (k + 1)], T.shw[:, 0:512].indirect(T.lo16[:, 32 * k:32 * k + 32]),
+                      T.msk[:, E * k:E * (k + 1)], A.mult, dep=[s_lo, l_sh, s_m[k]]))
     e_p = tt(T.pre[:], T.pa[:], T.pb[:], A.add, dep=[e_a, e_b])
+    c_om = ts(T.omask[:], T.oiota[:], T.of[:, 0:1], None, A.is_equal, dep=[i_o])
 
-    u = tt(T.uI[:], T.PS[:, 0:128], T.pixr[:], A.add, dep=[s_pe, e_r])
-    q = ts(T.qI[:], T.uI[:], 12, 3, A.arith_shift_right, A.bitwise_and, dep=[u])
-    c = ts(T.cI[:], T.uI[:], S - 1, None, A.bitwise_and)
-    for i in range(4):
-        n_i = ts(T.ind[:, 128 * i:128 * (i + 1)], T.qI[:], float(i), None, A.is_equal, dep=[q])
-    wait("t", n_i, c_1, c_2)
-    n_c = fin(g.tensor.matmul(T.PC[:], T.ONE[:], T.ind[:], True, True), "ct", 1)
-    n_m = fin(g.tensor.matmul(T.PM[:], T.M2[:], T.ind[:], True, True), "ct", 1)
-    cod = tt(T.cod[:], T.cI[:], T.pre[:], A.add, dep=[c, e_p])
-    for o in range(16):
-        x_all = act(T.X[:, o::16], T.cod[:], scale=T.omask[:, o:o + 1], dep=[cod, c_om])
-    wait("v", n_c, z_d2)
-    a = fin(g.vector.tensor_tensor_scan(T.scn[:], T.d0[:], T.PC[:], 1.0e4, A.min, A.add), "cv", 1)
-    a = tt(T.pos[:], T.scn[:], T.PM[:], A.add, dep=[a, n_m])
-    a = tt(T.m1[:], T.pos[:, 0:256], T.pos[:, 256:512], A.max, dep=[a])
-    a = tt(T.m2[:], T.m1[:, 0:128], T.m1[:, 128:256], A.max, dep=[a])
-    slot = ts(T.slot[:], T.m2[:], -BIG, None, A.add, dep=[a])
+    def shifts(h):
+        return to_lists(PS[h][:, 0:64], T.G, 1024 * h, 1024, [s_g[2 * h + 1], c_B])
+
+    def classes(h, s_pe, free):
+        cs = slice(64 * h, 64 * h + 64)
+        u = tt(T.uI[:, cs], PS[h][:, 0:64], T.pixr[:, cs], A.add, dep=[s_pe, e_r])
+        q = ts(T.qI[:, cs], T.uI[:, cs], 12, 3, A.arith_shift_right, A.bitwise_and, dep=[u])
+        c = ts(T.cI[:, cs], T.uI[:, cs], S - 1, None, A.bitwise_and)
+        for i in range(4):
+            n_i = ts(T.ind[:, 256 * h + 64 * i:256 * h + 64 * i + 64], T.qI[:, cs], float(i), None, A.is_equal, dep=[q])
+        wait("t", n_i, c_1, c_2, free)
+        ind = T.ind[:, 256 * h:256 * h + 256]
+        n_c = fin(g.tensor.matmul(T.PC[:, 0:256], T.ONE[:], ind, True, True), "ct", 1)
+        n_m = fin(g.tensor.matmul(T.PM[:, 0:256], T.M2[:], ind, True, True), "ct", 1)
+        codh = T["cod%d" % h]
+        cod = tt(codh[:], T.cI[:, cs], T.pre[:, cs], A.add, dep=[c, e_p])
+        xs = [act(T.X[:, E * (2 * h + i):E * (2 * h + i + 1)], codh[:, 0:64].indirect(T.rep[:, 32 * i:32 * i + 32]),
+                  dep=[cod, c_r]) for i in range(2)]
+        return n_c, n_m, xs
+
+    def slots(h, n_c, n_m):
+        c0 = 256 * h
+        wait("v", n_c, i_d)
+        a = fin(g.vector.tensor_tensor_scan(T.scn[:, c0:c0 + 256], T.d0[:], T.PC[:, 0:256], 1.0e4, A.min, A.add), "cv", 1)
+        p = tt(T.pos[:, c0:c0 + 256], T.scn[:, c0:c0 + 256], T.PM[:, 0:256], A.add, dep=[a, n_m])
+        a = tt(T.m1[:, 128 * h:128 * h + 128], T.pos[:, c0:c0 + 128], T.pos[:, c0 + 128:c0 + 256], A.max, dep=[p])
+        a = tt(T.m2[:, 64 * h:64 * h + 64], T.m1[:, 128 * h:128 * h + 64], T.m1[:, 128 * h + 64:128 * h + 128], A.max, dep=[a])
+        return ts(T.slot[:, 64 * h:64 * h + 64], T.m2[:, 64 * h:64 * h + 64], -BIG, None, A.add, dep=[a]), p
 
     PW = [T.PW0, T.PW1, T.PW2, T.PW3]
-    w_pe = []
-    for k in range(P):
-        a = cp(T.win[:, NL * k:NL * (k + 1)].indirect(T.slot[:, 32 * k:32 * k + 32]), T.X[:, E * k:E * (k + 1)],
-               dep=[slot, x_all, z_win[k]])
-        w_pe.append(to_lists(PW[k][:, 0:40], T.win, NL * k, NL, [a]))
+    w_pe = [None] * P
+
+    def bucket(k, dep):
+        return tt(T.win[:, NL * k:NL * (k + 1)].indirect(T.slot[:, 32 * k:32 * k + 32]), T.X[:, E * k:E * (k + 1)],
+                  T.omask[:], A.mult, dep=dep + [z_win[k], c_om])
+
+    def wrap(k, a):
+        w_pe[k] = to_lists(PW[k][:, 0:40], T.win, NL * k, NL, [a])
+
+    where = {k: (b, i) for b, ks in enumerate(BATCH) for i, k in enumerate(ks)}
+    ed, ee = ev_dst(r), ev_eng(r)
+    own_ev = [None] * len(BATCH)
 
     def out_lists(k):
-        if k == 0:
-            a = act(T.ev0[:, 0:30], PW[0][:, 0:30], dep=[w_pe[0]])
-            return a, act(T.land0[:, 3, 0:10], PW[0][:, 30:40])
-        a = act(T.ev1[:, :, 10 * k - 10:10 * k], PW[k][:, 0:30], dep=[w_pe[k]])
-        return a, act(T.land1[:, 3, 10 * k - 10:10 * k], PW[k][:, 30:40])
+        b, i = where[k]
+        a = act(T["ev%d" % b][:, :, 10 * i:10 * i + 10], PW[k][:, 0:30], dep=[w_pe[k]])
+        own_ev[b] = act(T["land%d" % b][:, 3, 10 * i:10 * i + 10], PW[k][:, 30:40])
+        if k == BATCH[b][-1]:
+            n = 10 * len(BATCH[b])
+            remote([(ed[j], ee[ed[j]], [T["ev%d" % b][:, j, :]], T["land%d" % b][:, j, 0:n]) for j in range(3)],
+                   "ev%d" % b, [a])
 
-    ed, ee = ev_dst(r), ev_eng(r)
-    a, own0 = out_lists(0)
-    remote([(ed[j], ee[ed[j]], [T.ev0[:, 10 * j:10 * j + 10]], T.land0[:, j, 0:10]) for j in range(3)], "evA", [a])
+    s0 = shifts(0)
+    n_c, n_m, xa = classes(0, s0, None)
+    s1 = shifts(1)
+    empty(2)
+    empty(3)
+    z_V = act(T.V[:, 0:NL], T.ttab[:, 0:NL], scale=0.0)
+    sa, free = slots(0, n_c, n_m)
+    b0 = bucket(0, [sa, xa[0]])
+    n_c, n_m, xb = classes(1, s1, free)
+    wrap(0, b0)
+    out_lists(0)
+    wrap(1, bucket(1, [xa[1]]))
+    sb, _ = slots(1, n_c, n_m)
     out_lists(1)
+    wrap(2, bucket(2, [sb, xb[0]]))
+    wrap(3, bucket(3, [xb[1]]))
     out_lists(2)
-
-    def nbrs(out, cin, dep):
-        for n, (d, lim, op) in enumerate(((-1.0, NL, A.max), (1.0, WN - 1, A.min), (-128.0, NL, A.max),
-                                          (128.0, WN - 1, A.min))):
-            tk = ts(out[:, :, 10 * n:10 * n + 10], cin, d, float(lim), A.add, op, dep=dep)
-        return tk
 
     def col(buf, k):
         return buf[:, 40 * k:40 * k + 40]
@@ -273,17 +292,28 @@ def rank_program(g, core, T, topo):
         return buf[:, NL * k:NL * (k + 1)]
 
     def nb(k, j, n=None):
-        buf, i = (T.nb0, j) if k == 0 else (T.nb1, 3 * j + k - 1)
+        b, i = where[k]
+        buf, i = T["nb%d" % b], len(BATCH[b]) * j + i
         return buf[:, i, :] if n is None else buf[:, i, 10 * n:10 * n + 10]
 
     d_t, d_c, d_p, d_n = [None] * P, [None] * P, [None] * P, [None] * P
-    x = cp(T.x0[:], T.land0[:, :, 0:10], dep=[("evA", n_ev), own0])
-    a = ts(T.t0[:], T.x0[:], 13, TT - 1, A.arith_shift_right, A.bitwise_and, dep=[x])
-    b = ts(T.c0[:], T.x0[:], 8191, None, A.bitwise_and)
-    d_t[0] = cp(col(T.t16, 0), T.t0[:], dep=[a])
-    d_p[0] = ts(col(T.p16, 0), T.x0[:], 0.0, None, A.is_lt)
-    d_c[0] = cp(col(T.cs16, 0), T.c0[:], dep=[b])
-    d_n[0] = nbrs(T.nb0, T.c0[:], [b])
+
+    def decode(b):
+        ks = BATCH[b]
+        xb_, tb, cb = T["x%d" % b], T["t%d" % b], T["c%d" % b]
+        x = cp(xb_[:], T["land%d" % b][:, :, 0:10 * len(ks)], dep=[("ev%d" % b, n_ev), own_ev[b]])
+        a = ts(tb[:], xb_[:], 13, TT - 1, A.arith_shift_right, A.bitwise_and, dep=[x])
+        c = ts(cb[:], xb_[:], 8191, None, A.bitwise_and)
+        for i, k in enumerate(ks):
+            cs = slice(10 * i, 10 * i + 10)
+            d_t[k] = cp(col(T.t16, k), tb[:, :, cs], dep=[a])
+            d_p[k] = ts(col(T.p16, k), xb_[:, :, cs], 0.0, None, A.is_lt)
+            d_c[k] = cp(col(T.cs16, k), cb[:, :, cs], dep=[c])
+        for n, (d, lim, op) in enumerate(((-1.0, NL, A.max), (1.0, WN - 1, A.min), (-128.0, NL, A.max),
+                                          (128.0, WN - 1, A.min))):
+            tk = ts(T["nb%d" % b][:, :, 10 * n:10 * n + 10], cb[:], d, float(lim), A.add, op)
+        for k in ks:
+            d_n[k] = tk
 
     tA, tW, tL, tE, tV, tS = ([None] * P for _ in range(6))
 
@@ -323,51 +353,50 @@ def rank_program(g, core, T, topo):
         out = ANS[k][:, 3 * CAP:3 * CAP + NL] if j == 3 else ag(k, j)
         return act(out, T.V[:, 0:WN].indirect(nb(k, j)), dep=[tS[k], d_n[k]])
 
-    def summed(k, j):
-        out = ANS[k][:, 3 * CAP:NL] if j == 3 else ag(k, j, 0)
-        tk = cp(out, T.V[:, 0:WN].indirect(nb(k, j, 0)), dep=[tS[k], d_n[k]])
-        for n in range(1, 4):
-            tk = tt(out, T.V[:, 0:WN].indirect(nb(k, j, n)), out, A.add, dep=[tk])
-        return tk
+    def summed(k, js, begun):
+        tk = dict(begun)
+        nxt = {j: 1 if j in begun else 0 for j in js}
+        while any(nxt[j] < 4 for j in js):
+            for j in js:
+                n = nxt[j]
+                if n < 4:
+                    src = T.V[:, 0:WN].indirect(nb(k, j, n))
+                    if n == 0:
+                        tk[j] = cp(ag(k, j, 0), src, dep=[tS[k], d_n[k]])
+                    else:
+                        tk[j] = tt(ag(k, j, 0), src, ag(k, j, 0), A.add, dep=[tS[k], tk[j]])
+                    nxt[j] = n + 1
+        return [tk[j] for j in js]
 
     ad, ae = an_dst(r), an_eng(r)
+    far = [j for j in range(3) if topo.chip(ad[j]) != topo.chip(core)]
+    near = [j for j in range(3) if j not in far]
 
-    def send(k, dep):
-        remote([(ad[j], ae[ad[j]], [ag(k, j, n) for n in range(4)], ANS[k][:, CAP * j:CAP * (j + 1)]) for j in range(3)],
-               "an%d" % k, dep)
+    def send(k, dep, sums=()):
+        remote([(ad[j], ae[ad[j]], [ag(k, j, 0)] if j in sums else [ag(k, j, n) for n in range(4)],
+                 ANS[k][:, CAP * j:CAP * (j + 1)]) for j in range(3)], "an%d" % k, dep)
 
-    def own_sum(k, dep):
+    def own_dma(k, dep):
         a = dma("g", ANS[k][:, 480:800], ANS[k][:, 800:1120], "accA", dep=dep, accum_op=A.add)
         return dma("g", ANS[k][:, 480:640], ANS[k][:, 640:800], "accB%d" % k, dep=[a], accum_op=A.add)
 
     def pick(q, k, c0, c1, dep):
         out = T.yst[:, E * k + 16 * c0:E * k + 16 * c1]
         src = ANS[k][:, 0:NL].indirect(T.slot[:, 32 * k + c0:32 * k + c1])
-        return cp(out, src, dep=dep) if q == "v" else act(out, src, dep=dep)
+        return cp(out, src, dep=dep) if q == "v" else act(out, src, dep=dep + [sb])
 
-    def store(k, dep):
-        return dma("y", T.y[:, E * k:E * (k + 1)], T.yst[:, E * k:E * (k + 1)], "st", dep=dep)
+    def store(q, c0, c1, dep):
+        return dma(q, T.y[:, c0:c1], T.yst[:, c0:c1], "st", dep=dep)
 
+    decode(0)
     times(0)
-    a, own1 = out_lists(3)
-    remote([(ed[j], ee[ed[j]], [T.ev1[:, j, :]], T.land1[:, j, 0:30]) for j in range(3)], "evB", [a])
+    out_lists(3)
     pols(0)
     get_last(0)
     decay(0)
     put_last(0)
+    decode(1)
     get_state(0)
-
-    x = cp(T.x1[:], T.land1[:, :, 0:30], dep=[("evB", n_ev), own1])
-    a1 = ts(T.t1[:], T.x1[:], 13, TT - 1, A.arith_shift_right, A.bitwise_and, dep=[x])
-    b1 = ts(T.c1[:], T.x1[:], 8191, None, A.bitwise_and)
-
-    def lists(k):
-        cs = slice(10 * k - 10, 10 * k)
-        d_t[k] = cp(col(T.t16, k), T.t1[:, :, cs], dep=[a1])
-        d_p[k] = ts(col(T.p16, k), T.x1[:, :, cs], 0.0, None, A.is_lt)
-        d_c[k] = cp(col(T.cs16, k), T.c1[:, :, cs], dep=[b1])
-
-    lists(1)
     put_state(0, [])
     times(1)
     pols(1)
@@ -376,55 +405,42 @@ def rank_program(g, core, T, topo):
         get_last(k + 1)
         four(k, 0)
         decay(k + 1)
-        if k == 0:
-            lists(2)
-            lists(3)
-            d_n[1] = d_n[2] = d_n[3] = nbrs(T.nb1, T.c1[:], [b1])
         put_last(k + 1)
+        if k == 0:
+            decode(2)
         get_state(k + 1)
         four(k, 1)
         a = four(k, 2)
         send(k, [a])
         a = four(k, 3)
-        own[k] = own_sum(k, [a])
+        own[k] = own_dma(k, [a])
         put_state(k + 1, [a])
         times(k + 2)
         pols(k + 2)
     get_last(3)
-    four(2, 0)
+    nr = [four(2, j) for j in near]
     decay(3)
-    own[2] = summed(2, 3)
+    o2 = four(2, 3)
+    sm = summed(2, far, {})
     get_state(3)
-    four(2, 1)
-    a = four(2, 2)
-    send(2, [a])
-    y0 = pick("v", 0, 0, 32, [("an0", n_an), own[0]])
-    store(0, [y0])
-    put_state(3, [a])
-    y1 = pick("s", 1, 0, 32, [("an1", n_an), own[1]])
-    store(1, [y1])
+    send(2, sm + nr, far)
+    put_state(3, [o2] + sm)
+    store("y", 0, E, [pick("s", 0, 0, 32, [("an0", n_an), own[0]])])
 
-    far, near, first, second, te = tail_plan(r)
-    done = {}
-    for j in far:
-        done[j] = summed(3, j)
-    for j in near:
-        done[j] = four(3, j)
-    a = four(3, 3)
-
-    def tail(js):
-        remote([(ad[j], te[ad[j]], [ag(3, j, 0)] if j in far else [ag(3, j, n) for n in range(4)],
-                 ANS[3][:, CAP * j:CAP * (j + 1)]) for j in js], "an3", [done[j] for j in js])
-
-    tail(first)
-    tail(second)
-    a = tt(ANS[3][:, 480:800], ANS[3][:, 480:800], ANS[3][:, 800:1120], A.add, dep=[a])
-    own[3] = tt(ANS[3][:, 480:640], ANS[3][:, 480:640], ANS[3][:, 640:800], A.add, dep=[a])
-    y2 = pick("s", 2, 0, 32, [("an2", n_an), own[2]])
-    store(2, [y2])
-    ya = pick("v", 3, 0, 16, [("an3", n_tail), own[3]])
-    yb = pick("s", 3, 16, 32, [("an3", n_tail), own[3]])
-    a = store(3, [ya, yb])
+    begun = {j: act(ag(3, j, 0), T.V[:, 0:WN].indirect(nb(3, j, 0)), dep=[tS[3], d_n[3]]) for j in far[1:]}
+    nr = [four(3, j) for j in near]
+    o3 = four(3, 3)
+    sm = summed(3, far, begun)
+    send(3, sm + nr, far)
+    half = [tt(ANS[k][:, 480:800], ANS[k][:, 480:800], ANS[k][:, 800:1120], A.add, dep=[o]) for k, o in ((2, o2), (3, o3))]
+    for k in (2, 3):
+        own[k] = tt(ANS[k][:, 480:640], ANS[k][:, 480:640], ANS[k][:, 640:800], A.add, dep=[half[k - 2]])
+    for k in (1, 2):
+        store("y", E * k, E * (k + 1), [pick("s", k, 0, 32, [("an%d" % k, n_an), own[k]])])
+    ya = pick("v", 3, 0, 16, [("an3", n_an), own[3]])
+    yb = pick("s", 3, 16, 32, [("an3", n_an), own[3]])
+    store("y", E * 3, E * 3 + 256, [ya])
+    a = store("s", E * 3 + 256, E * 4, [yb])
     wait("y", a)
     for s, n in cnt.items():
         if max(waited[q].get(s, 0) for q in Q) < n:

@@ -4,9 +4,16 @@ from concourse.mybir import ActivationFunctionType as F
 
 P, E, S, TT, CAP = 4, 512, 4096, 2048, 160
 NL = 4 * CAP
-WN = NL + S
+WN = S + 3 * 256 + CAP
+WK = 7 * CAP
+AK = 3 * CAP + 4 * NL
 BIG = 1025.0
-BATCH = [[0], [1], [2, 3]]
+T_HI, T_LO, PIX_HI, PIX_LO = 2, 6, 7, 9
+SRC = [[0], [1], [2, 3]]
+DEC = [[0], [1], [2], [3]]
+L_S = TT + 1024
+SM_S, SM_G = 11, 11
+BF = "bfloat16"
 
 
 def _sb(cols, dt="float32"):
@@ -14,35 +21,40 @@ def _sb(cols, dt="float32"):
 
 
 SCRATCH = {
-    "tmI": _sb(128, "int32"), "pixI": _sb(128, "int32"), "polI": _sb(128, "int32"), "shw": _sb(512, "int32"),
-    "ratec": _sb(4), "ttab": _sb(TT), "pI": _sb(4, "int32"), "oI": _sb(4, "int32"), "pf": _sb(4), "of": _sb(4),
-    "gf": _sb(4), "iotaE": _sb(32), "Etab": _sb(32), "blk": _sb(128), "Bm": _sb(144),
-    "oiota": _sb(E), "omask": _sb(E), "rep": _sb(128, "uint16"),
-    "ONE": _sb(128, "bfloat16"), "M2": _sb(128, "bfloat16"), "k1": _sb(128), "k2": _sb(128), "k3": _sb(128),
-    "d0": _sb(256), "wtab": _sb(8),
-    "hI": _sb(128, "int32"), "loI": _sb(128, "int32"), "h16": _sb(128, "uint16"), "lo16": _sb(128, "uint16"),
-    "msk": _sb(P * E), "G": _sb(P * E), "X": _sb(P * E), "win": _sb(P * NL),
-    "pa": _sb(128), "pb": _sb(128), "pre": _sb(128), "pixr": _sb(128),
-    "uI": _sb(128, "int32"), "qI": _sb(128, "int32"), "cI": _sb(128, "int32"), "cod0": _sb(64), "cod1": _sb(64),
-    "ind": _sb(512, "bfloat16"), "scn": _sb(512), "pos": _sb(512), "m1": _sb(256), "m2": _sb(128),
-    "slot": _sb(128, "uint16"),
-    "cs16": _sb(160, "uint16"), "t16": _sb(160, "uint16"), "p16": _sb(160, "uint16"),
-    "V": _sb(WN), "L": _sb(WN, "int32"), "Ld": ("dram", [8, 4, S], "int32"),
-    "At": _sb(P * NL), "Wt": _sb(P * NL), "dt": _sb(P * NL), "Ex": _sb(P * NL), "tmp": _sb(P * NL),
-    "ag": _sb(P * 3 * NL), "ans0": _sb(1120), "ans1": _sb(1120), "ans2": _sb(1120), "ans3": _sb(1120),
+    "tmI": _sb(128, "int32"), "pixI": _sb(128, "int32"), "polI": _sb(128, "int32"),
+    "lastI": _sb(256, "int32"), "ratec": _sb(4), "s0I": _sb(256, "int32"), "s1I": _sb(256, "int32"),
+    "lastH": _sb(256, BF), "lastL": _sb(256, BF),
+    "zp": _sb(128), "zI": _sb(128), "zH": _sb(128, BF), "zL": _sb(128, BF), "pixr": _sb(128), "t16": _sb(128, "uint16"),
+    "pI": _sb(4, "int32"), "oI": _sb(4, "int32"), "col": _sb(8), "m16": _sb(16), "gm": _sb(4), "gn": _sb(4),
+    "gb": _sb(4), "eb": _sb(4), "io8": _sb(8), "cnt": _sb(CAP, BF), "blk": _sb(128, BF), "tH": _sb(128, BF),
+    "Bf": _sb(144, BF), "Bm": _sb(144, BF), "NEG": _sb(128, BF), "M1": _sb(128, BF), "M2": _sb(128, BF),
+    "Dsel": _sb(128, BF), "Wsel": _sb(128, BF), "Sm": _sb([16, 130], BF),
+    "G": _sb(P * E, BF), "Y": _sb(P * E, BF), "Id": _sb(128),
+    "W": _sb(P * WK, BF),
+    "uI": _sb(128, "int32"), "qI": _sb(128, "int32"), "slot": _sb(128, "uint16"),
+    "xI": _sb([P, 40], "int32"), "cI": _sb([P, 40], "int32"), "c16": _sb([P, 40], "uint16"), "nb": _sb([P, 160], "uint16"),
+    "V": _sb(WN), "L": _sb(WN, BF), "Lg": _sb(P * NL, BF), "Ex": _sb(P * NL), "W2": _sb(P * NL), "tmp": _sb(P * NL),
     "yst": _sb(P * E),
+    "PA": ("psum", [128, 1024], "float32"), "PB": ("psum", [128, 1024], "float32"),
 }
-for _b, _ks in enumerate(BATCH):
-    _n = 10 * len(_ks)
-    SCRATCH["ev%d" % _b] = _sb([3, _n])
-    SCRATCH["land%d" % _b] = _sb([4, (_n + 3) // 4 * 4])
-    for _x in "xct":
-        SCRATCH["%s%d" % (_x, _b)] = _sb([4, _n], "int32")
-    SCRATCH["nb%d" % _b] = _sb([4 * len(_ks), 40], "uint16")
-for _x in ("PS0", "PS1", "PC", "PM", "PW0", "PW1", "PW2", "PW3"):
+for _k in range(P):
+    SCRATCH["an%d" % _k] = _sb(AK)
+for _b, _ks in enumerate(SRC):
+    _n = 32 * len(_ks)
+    SCRATCH.update({"d%d" % _b: _sb(4 * _n), "ind%d" % _b: _sb(4 * _n, BF), "scn%d" % _b: _sb(4 * _n),
+                    "pos%d" % _b: _sb(4 * _n), "ma%d" % _b: _sb(2 * _n), "mb%d" % _b: _sb(_n)})
+for _x in ("PS0", "PS1", "PC", "PM"):
     SCRATCH[_x] = ("psum", [128, 512], "float32")
-SEMAPHORES = ["cv", "cs", "ct", "cg", "ltm", "lsh", "lpp", "lD", "lL", "lv", "lrate", "ev0", "ev1", "ev2",
-              "an0", "an1", "an2", "an3", "sent", "accA", "accB0", "accB1", "st"]
+SEMAPHORES = ["cv", "cs", "ct", "cg", "ltm", "lsh", "lpix", "lpol", "llast", "lv", "lrate", "rowB", "rowC", "rowL", "cpW", "ls0",
+              "sent", "st"] + ["%s%d" % (_x, _k) for _x in ("ev", "an") for _k in range(P)]
+
+NBR = [[(0, 4, "s")], [(0, 4, "s")], [(2, 4, "v"), (0, 2, "s")], [(2, 3, "v"), (3, 4, "v"), (1, 2, "s"), (0, 1, "s")]]
+SENDS = [[[1, 2, 3]]] * 3 + [[[1, 2], [3]]]
+PICK = [[("s", 0, 32)]] * 3 + [[("v", 0, 16), ("s", 16, 32)]]
+
+
+def seq(pat, xs):
+    return [pat % x for x in xs]
 
 
 def _bits(es):
@@ -74,374 +86,340 @@ def rank_program(g, core, T, topo):
     cores = list(T.cores)
     N = len(cores)
     Q = {"v": g.vector, "s": g.scalar, "t": g.tensor, "g": g, "y": g.sync}
-    cnt = {}
-    waited = {q: {} for q in Q}
+    V, SC, PE = g.vector, g.scalar, g.tensor
+    ops = {}
 
-    def wait(q, *toks):
-        for tk in toks:
-            if tk is None:
-                continue
-            s, n = tk
-            if waited[q].get(s, 0) < n:
-                Q[q].wait_ge(T.sem[s], n)
-                waited[q][s] = n
+    def op(name, q, fn, dep=(), sem=None):
+        ops[name] = (q, fn, list(dep), sem)
 
-    def fin(ins, s, n):
-        ins.then_inc(T.sem[s], n)
-        cnt[s] = cnt.get(s, 0) + n
-        return (s, cnt[s])
-
-    def ts(out, in0, s1, s2, op0, op1=None, dep=()):
-        wait("v", *dep)
+    def ts(name, out, in0, s1, s2, op0, op1=None, dep=()):
         if op1 is None:
-            return fin(g.vector.tensor_scalar(out, in0, s1, None, op0), "cv", 1)
-        return fin(g.vector.tensor_scalar(out, in0, s1, s2, op0, op1), "cv", 1)
+            op(name, "v", lambda: V.tensor_scalar(out, in0, s1, None, op0), dep)
+        else:
+            op(name, "v", lambda: V.tensor_scalar(out, in0, s1, s2, op0, op1), dep)
 
-    def tt(out, in0, in1, op, dep=()):
-        wait("v", *dep)
-        return fin(g.vector.tensor_tensor(out, in0, in1, op), "cv", 1)
+    def tt(name, out, in0, in1, o, dep=()):
+        op(name, "v", lambda: V.tensor_tensor(out, in0, in1, o), dep)
 
-    def cp(out, in_, dep=()):
-        wait("v", *dep)
-        return fin(g.vector.tensor_copy(out, in_), "cv", 1)
+    def cp(name, out, in_, dep=()):
+        op(name, "v", lambda: V.tensor_copy(out, in_), dep)
 
-    def ms(ap, c, dep=()):
-        wait("v", *dep)
-        return fin(g.vector.memset(ap, c), "cv", 1)
+    def act(name, out, in_, dep=(), func=F.Identity, **kw):
+        op(name, "s", lambda: SC.activation(out, in_, func, **kw), dep)
 
-    def act(out, in_, func=F.Identity, dep=(), **kw):
-        wait("s", *dep)
-        return fin(g.scalar.activation(out, in_, func, **kw), "cs", 1)
+    def iota(name, out, pat, base=0, cm=0):
+        op(name, "g", lambda: g.iota(out, pat, base, cm, allow_small_or_imprecise_dtypes=True))
 
-    def iota(out, pat, base, cm, flag=True):
-        if flag:
-            return fin(g.iota(out, pat, base, cm, allow_small_or_imprecise_dtypes=True), "cg", 1)
-        return fin(g.iota(out, pat, base, cm), "cg", 1)
+    def dma(name, q, out, in_, sem, dep=(), **kw):
+        op(name, q, lambda: Q[q].dma_start(out, in_, **kw), dep, sem)
 
-    def dma(q, out, in_, s, dep=(), **kw):
-        wait(q, *dep)
-        return fin(Q[q].dma_start(out, in_, **kw), s, 16)
+    def mm(name, items, dep):
+        def fn():
+            for out, lhsT, rhs, start, stop in items:
+                ins = PE.matmul(out, lhsT, rhs, start, stop)
+            return ins
+        op(name, "t", fn, dep)
 
-    def to_lists(out, buf, c0, n, dep):
-        wait("t", *dep)
-        for o in range(16):
-            ins = g.tensor.matmul(out, T.Bm[:, 15 - o:143 - o], buf[:, c0 + o:c0 + n:16], o == 0, o == 15)
-        return fin(ins, "ct", 1)
+    def to_lists(name, out, buf, c0, n, dep):
+        mm(name, [(out, T.Bm[:, 15 - o:143 - o], buf[:, c0 + o:c0 + n:16], o == 0, o == 15) for o in range(16)], dep + ["Bm"])
 
-    def remote(items, sem, dep):
-        wait("g", *dep)
-        trs, tot = [], 0
+    sent = [0]
+
+    def remote(name, items, sem, dep):
+        trs = []
         for d, es, srcs, dst in items:
             rid, pid, _ = topo.addr(d)
             trs.append(RemoteDMATransfer(dst_ids=[DstId(rid=rid, pnc=pid)], dma_engine_mask=_bits(es),
                                          remote_sem=T.sem[sem], srcs=srcs, dsts=[dst], alu_op=1 if len(srcs) > 1 else 0))
-            tot += len(es)
-        g.remote_dma_fused(trs, local_sem=T.sem.sent)
-        cnt["sent"] = cnt.get("sent", 0) + tot
+            sent[0] += len(es)
+        op(name, "g", lambda: g.remote_dma_fused(trs, local_sem=T.sem.sent), dep, "remote")
 
-    def ev_dst(a):
-        return [cores[(a + 3 - j) % N] for j in range(3)]
+    def senders(a):
+        rest = [b for b in range(N) if b != a]
+        return [a] + sorted(rest, key=lambda b: topo.chip(cores[b]) != topo.chip(cores[a]))
 
-    def an_dst(a):
-        return [cores[(a - 3 + j) % N] for j in range(3)]
+    def bucket(src, a):
+        return 3 - (a - src) % N
 
-    def ev_eng(a):
-        return _share(topo, cores[a], ev_dst(a), 4)
+    def engines(a, calls):
+        out = {}
+        for ps in calls:
+            out.update(_share(topo, cores[a], [cores[senders(a)[p]] for p in ps], 8))
+        return out
 
-    def an_eng(a):
-        return _share(topo, cores[a], an_dst(a), 16)
-
-    others = [a for a in range(N) if a != r]
-    n_ev = sum(len(ev_eng(a)[core]) for a in others)
-    n_an = sum(len(an_eng(a)[core]) for a in others)
-
-    l_tm = dma("y", T.tmI[:], T.tm[:], "ltm")
-    l_sh = dma("s", T.shw[:], T.sh[:], "lsh")
-    dma("y", T.pixI[:], T.pix[:], "lpp")
-    l_pp = dma("y", T.polI[:], T.pol[:], "lpp")
-    for x in range(4):
-        l_D = dma("s" if x < 2 else "y", T.Ld[:, x, :], T.last[:], "lD")
-    for m in range(4):
-        l_L = dma("y", T.L[m::4, NL:WN], T.Ld[:], "lL", dep=[l_D])
-
-    i_p = iota(T.pI[:, 0:1], [[0, 1]], 0, 1, False)
-    i_e = iota(T.iotaE[:], [[4, 4], [1, 8]], 0, 0)
-    i_ta = iota(T.ttab[:, 0:144], [[1, 144]], 0, 0)
-    i_b = iota(T.blk[:], [[16, 8], [0, 16]], 0, 0)
-    i_t0 = iota(T.ttab[:, 144:NL], [[1, NL - 144]], 144, 0)
-    i_o = iota(T.oiota[:], [[0, 32], [1, 16]], 0, 0)
-    i_d = iota(T.d0[:], [[-CAP, 4], [0, 2], [1000, 32]], 3 * CAP, 0)
-    l_v = dma("g", T.V[:, NL:WN], T.v[:], "lv")
-    l_rate = dma("g", T.ratec[:, 0:1], T.rate[:], "lrate", allow_slow_non_contiguous=True)
-    i_t1 = iota(T.ttab[:, NL:TT], [[1, TT - NL]], NL, 0)
-
-    z_w = ms(T.wtab[:], 1.0)
-    z_L = ms(T.L[:, 0:NL], 0)
-    c_o = ts(T.oI[:, 0:1], T.pI[:, 0:1], 15, None, A.bitwise_and, dep=[i_p])
-    c_p = cp(T.pf[:, 0:1], T.pI[:, 0:1])
-    z_w = ms(T.wtab[:, 1:2], -1.0, dep=[z_w])
-    c_of = cp(T.of[:, 0:1], T.oI[:, 0:1], dep=[c_o])
-    a = ts(T.k1[:], T.ttab[:, 0:128], T.pf[:, 0:1], -1.0, A.is_lt, A.mult, dep=[c_p, i_ta])
-    c_g = tt(T.gf[:, 0:1], T.pf[:, 0:1], T.of[:, 0:1], A.subtract, dep=[c_of])
-    c_E = ts(T.Etab[:], T.iotaE[:], T.of[:, 0:1], None, A.is_equal, dep=[i_e])
-    b = ts(T.k3[:], T.ttab[:, 0:128], T.pf[:, 0:1], BIG - 1.0, A.is_equal, A.mult)
-    c_1 = ts(T.ONE[:], T.blk[:], T.gf[:, 0:1], None, A.is_equal, dep=[i_b, c_g])
-    c_B = ts(T.Bm[:], T.ttab[:, 0:144], -15.0, T.gf[:, 0:1], A.add, A.is_equal)
-    a = tt(T.k2[:], T.k1[:], T.ONE[:], A.mult, dep=[a, c_1])
-    c_r = cp(T.rep[:, 0:64], T.ttab[:, 0:64])
-
-    z_win = [None] * P
-
-    def empty(k):
-        z_win[k] = act(T.win[:, NL * k:NL * (k + 1)], T.ttab[:, 0:NL], scale=1.0 / 16, dep=[i_t0])
-
-    a1 = ts(T.hI[:], T.tmI[:], 9, None, A.arith_shift_right, dep=[l_tm])
-    b1 = ts(T.loI[:], T.tmI[:], 511, None, A.bitwise_and)
-    s_h = cp(T.h16[:], T.hI[:], dep=[a1])
-    s_lo = cp(T.lo16[:], T.loI[:], dep=[b1])
-    s_m = [act(T.msk[:, E * k:E * (k + 1)], T.Etab[:, 8 * k:8 * k + 8].indirect(T.h16[:, 32 * k:32 * k + 32]),
-               dep=[s_h, c_E]) for k in range(P)]
-    empty(0)
-    empty(1)
-    c_2 = tt(T.M2[:], T.k2[:], T.k3[:], A.add, dep=[a, b])
-    e_a = ts(T.pa[:], T.tmI[:], 8192.0, float(NL - 2 ** 23), A.mult, A.add)
-    e_b = ts(T.pb[:], T.polI[:], float(2 ** 23), None, A.mult, dep=[l_pp])
-    e_r = ts(T.pixr[:], T.pixI[:], float(S * ((N - r) % N)), None, A.add)
-    PS = [T.PS0, T.PS1]
-    s_g = []
+    others = senders(r)[1:]
+    arrive = {}
     for k in range(P):
-        s_g.append(tt(T.G[:, E * k:E * (k + 1)], T.shw[:, 0:512].indirect(T.lo16[:, 32 * k:32 * k + 32]),
-                      T.msk[:, E * k:E * (k + 1)], A.mult, dep=[s_lo, l_sh, s_m[k]]))
-    e_p = tt(T.pre[:], T.pa[:], T.pb[:], A.add, dep=[e_a, e_b])
-    c_om = ts(T.omask[:], T.oiota[:], T.of[:, 0:1], None, A.is_equal, dep=[i_o])
+        arrive["ev%d" % k] = sum(len(engines(a, [[1, 2, 3]])[core]) for a in others)
+        arrive["an%d" % k] = sum(len(engines(a, SENDS[k])[core]) for a in others)
 
-    def shifts(h):
-        return to_lists(PS[h][:, 0:64], T.G, 1024 * h, 1024, [s_g[2 * h + 1], c_B])
+    dma("l_s0", "y", T.s0I[:], T.sh[:, 0:2 * TT], "ls0")
+    dma("l_s1", "y", T.s1I[:], T.sh[:, 2 * TT:4 * TT], "lsh")
+    dma("l_tm", "s", T.tmI[:], T.tm[:], "ltm")
+    dma("l_pix", "s", T.pixI[:], T.pix[:], "lpix")
+    dma("l_pol", "s", T.polI[:], T.pol[:], "lpol")
+    dma("l_last", "y", T.lastI[:], T.last[:], "llast")
+    for h in range(2):
+        dma("l_v%d" % h, "y", T.V[:, S // 2 * h:S // 2 * (h + 1)], T.v[:, S // 2 * h:S // 2 * (h + 1)], "lv")
+    dma("l_rate", "y", T.ratec[:, 0:1], T.rate[:], "lrate")
 
-    def classes(h, s_pe, free):
-        cs = slice(64 * h, 64 * h + 64)
-        u = tt(T.uI[:, cs], PS[h][:, 0:64], T.pixr[:, cs], A.add, dep=[s_pe, e_r])
-        q = ts(T.qI[:, cs], T.uI[:, cs], 12, 3, A.arith_shift_right, A.bitwise_and, dep=[u])
-        c = ts(T.cI[:, cs], T.uI[:, cs], S - 1, None, A.bitwise_and)
+    pf, of, gf, mT, mU, t128 = (T.col[:, i:i + 1] for i in range(6))
+    op("i_p", "g", lambda: g.iota(T.pI[:, 0:1], [[0, 1]], 0, 1))
+    iota("i_cnt", T.cnt[:], [[1, CAP]])
+    iota("i_blk", T.blk[:], [[16, 8], [0, 16]])
+    iota("i_k", T.io8[:, 0:4], [[TT, 4]])
+    iota("i_e", T.io8[:, 4:8], [[256 - S, 4]], S * (r + 4))
+    for b, ks in enumerate(SRC):
+        iota("i_d%d" % b, T["d%d" % b][:], [[-CAP, 4], [0, len(ks)], [1000, 32]], 3 * CAP)
+    iota("z_V", T.V[:, S:WN], [[0, WN - S]])
+    iota("z_Lg", T.L[:, L_S + CAP:WN], [[0, WN - L_S - CAP]])
+    op("z_B", "v", lambda: V.memset(T.L[:, 0:TT], 0.0))
+    act("z_Ls", T.L[:, L_S:L_S + CAP], T.cnt[:], ["i_cnt"], F.Exp, scale=0.0)
+    ts("oI", T.oI[:, 0:1], T.pI[:, 0:1], 15, None, A.bitwise_and, dep=["i_p"])
+    cp("pf", pf, T.pI[:, 0:1], ["i_p"])
+    cp("of", of, T.oI[:, 0:1], ["oI"])
+    tt("gf", gf, pf, of, A.subtract, ["pf", "of"])
+    ts("m16", T.m16[:], T.cnt[:, 0:16], of, None, A.is_equal, dep=["of", "i_cnt"])
+
+    def m(o):
+        return T.m16[:, o:o + 1]
+
+    ts("Bf", T.Bf[:], T.cnt[:, 0:144], -15.0, gf, A.add, A.is_equal, dep=["gf", "i_cnt"])
+    ts("eb", T.eb[:], T.io8[:, 4:8], m(PIX_HI), None, A.mult, dep=["m16", "i_e"])
+    tt("mT", mT, m(T_HI), m(T_LO), A.add, ["m16"])
+    ts("mU", mU, mT, 0.0, None, A.is_equal, dep=["mT"])
+    ts("t128", t128, m(T_HI), 127.0, mT, A.mult, A.add, dep=["mT"])
+    tt("gn", T.gn[:], T.m16[:, 0:16:4], T.m16[:, 1:16:4], A.add, ["m16"])
+    ts("gm", T.gm[:], T.gn[:], t128, None, A.add, dep=["gn", "t128"])
+    ts("gb", T.gb[:], T.io8[:, 0:4], m(T_HI), None, A.mult, dep=["m16", "i_k"])
+    ts("NEG", T.NEG[:], T.blk[:], gf, -1.0, A.is_equal, A.mult, dep=["gf", "i_blk"])
+    ts("Id", T.Id[:], T.cnt[:, 0:128], pf, None, A.is_equal, dep=["pf", "i_cnt"])
+    op("M1", "g", lambda: g.affine_select(T.M1[:], T.NEG[:], [[-1, 128]], A.is_gt, 0.0, 0, 1), ["NEG"])
+    op("M2", "g", lambda: g.affine_select(T.M2[:], T.M1[:], [[-1, 128]], A.not_equal, BIG - 1.0, 0, 1), ["M1"])
+    act("tH", T.tH[:], T.cnt[:, 0:128], ["of", "i_cnt"], scale=0.0, bias=of)
+    act("Bm", T.Bm[:], T.Bf[:], ["Bf", "mU"], scale=mU)
+    act("Dsel", T.Dsel[:], T.NEG[:], ["NEG", "mT"], scale=mT)
+    act("Wsel", T.Wsel[:], T.NEG[:], ["NEG", "m16"], scale=m(PIX_HI))
+    for j in range(16):
+        src = T.Bf[:, 15 - PIX_LO:145 - PIX_LO]
+        if j >= SM_G:
+            op("Sm%d" % j, "g", lambda j=j, src=src: g.affine_select(T.Sm[:, j, :], src, [[1, 130]], A.is_equal, 0.0,
+                                                                     j - PIX_LO, -1), ["Bf"])
+        elif j < SM_S:
+            act("Sm%d" % j, T.Sm[:, j, :], src, ["Bf", "m16"], scale=m(j))
+        else:
+            ts("Sm%d" % j, T.Sm[:, j, :], src, m(j), None, A.mult, dep=["Bf", "m16"])
+    for k in range(2):
+        for j in range(4):
+            act("E%d%d" % (k, j), T.W[:, WK * k + CAP * j:WK * k + CAP * (j + 1)], T.cnt[:], ["eb", "i_cnt"],
+                scale=m(PIX_LO), bias=T.eb[:, j:j + 1])
+    for k in range(2, P):
+        dma("cpW%d" % k, "y", T.W[:, WK * k:WK * k + NL], T.W[:, WK:WK + NL], "cpW", seq("E1%d", range(4)))
+
+    part = {x + y: T.L[:, TT + 256 * i:TT + 256 * (i + 1)] for i, (x, y) in enumerate(("0H", "0L", "1H", "1L"))}
+    ts("zp", T.zp[:], T.polI[:], 16384.0, -16384.0, A.mult, A.add, dep=["l_pol"])
+    tt("zI", T.zI[:], T.pixI[:], T.zp[:], A.add, ["zp", "l_pix"])
+    for x, ld in (("s0", "l_s0"), ("s1", "l_s1"), ("last", "l_last"), ("z", "zI")):
+        hi, lo = (part[x[1] + "H"], part[x[1] + "L"]) if x[0] == "s" else (T[x + "H"][:], T[x + "L"][:])
+        cp(x + "H", hi, T[x + "I"][:], [ld])
+        tt(x + "L", lo, T[x + "I"][:], hi, A.subtract, [x + "H"])
+    cp("t16", T.t16[:], T.tmI[:], ["l_tm"])
+    ts("pixr", T.pixr[:], T.pixI[:], float(S * ((N - r) % N)), None, A.add, dep=["l_pix"])
+    dma("r_tH", "y", T.L[T_HI::16, 0:TT], T.tH[:], "rowB", ["z_B", "tH"])
+    dma("r_tL", "y", T.L[T_LO::16, 0:TT], T.cnt[:, 0:128], "rowB", ["z_B", "i_cnt"])
+    dma("r_s0H", "y", T.L[0::8, 0:TT], part["0H"], "rowB", ["z_B", "s0H"])
+    dma("r_s0L", "y", T.L[1::8, 0:TT], part["0L"], "rowB", ["z_B", "s0L"])
+    dma("r_s1H", "y", T.L[4::8, 0:TT], part["1H"], "rowC", ["G0", "G1", "s1H"])
+    dma("r_s1L", "y", T.L[5::8, 0:TT], part["1L"], "rowC", ["G0", "G1", "s1L"])
+    dma("r_lH", "y", T.L[T_HI::16, 0:S], T.lastH[:], "rowL", ["z_Lg", "z_Ls", "lastH"] + seq("G%d", range(P)))
+    dma("r_lL", "y", T.L[T_LO::16, 0:S], T.lastL[:], "rowL", ["z_Lg", "z_Ls", "lastL"] + seq("G%d", range(P)))
+
+    PY = [T.PA, T.PB]
+    PS = [T.PS0, T.PS1]
+    for k in range(P):
+        es, ls, c0 = slice(E * k, E * (k + 1)), slice(32 * k, 32 * k + 32), E * (k % 2)
+        act("G%d" % k, T.G[:, es], T.L[:, 0:TT].indirect(T.t16[:, ls]), ["r_s%dL" % (k // 2), "t16", "gm", "gb"],
+            scale=T.gm[:, 2 * (k % 2) + k // 2:2 * (k % 2) + k // 2 + 1], bias=T.gb[:, k:k + 1])
+        for h in range(2):
+            js = range(8 * h, 8 * h + 8)
+            mm("y%d%d" % (k, h), [(PY[k // 2][:, c0 + j:c0 + E:16], T.Sm[:, j, PIX_LO - row:PIX_LO - row + 128], T[f][:, ls],
+                                   i == 0, i == 1) for j in js for i, (f, row) in enumerate((("zH", PIX_HI), ("zL", PIX_LO)))],
+               seq("Sm%d", js) + ["zH", "zL"])
+        act("Y%d" % k, T.Y[:, es], PY[k // 2][:, c0:c0 + E], seq("y%d%%d" % k, range(2)))
+    counted = {}
+    for b, ks in enumerate(SRC):
+        n, x = 32 * len(ks), str(b)
+        ls = slice(32 * ks[0], 32 * ks[0] + n)
+        ind, scn, pos, ma, mb = (T[y + x] for y in ("ind", "scn", "pos", "ma", "mb"))
+        to_lists("sh" + x, PS[b % 2][:, 0:n], T.G, E * ks[0], 16 * n, seq("G%d", ks) + (["u%d" % (b - 2)] if b > 1 else []))
+        tt("u" + x, T.uI[:, ls], PS[b % 2][:, 0:n], T.pixr[:, ls], A.add, ["sh" + x, "pixr"])
+        ts("q" + x, T.qI[:, ls], T.uI[:, ls], 12, 3, A.arith_shift_right, A.bitwise_and, dep=["u" + x])
         for i in range(4):
-            n_i = ts(T.ind[:, 256 * h + 64 * i:256 * h + 64 * i + 64], T.qI[:, cs], float(i), None, A.is_equal, dep=[q])
-        wait("t", n_i, c_1, c_2, free)
-        ind = T.ind[:, 256 * h:256 * h + 256]
-        n_c = fin(g.tensor.matmul(T.PC[:, 0:256], T.ONE[:], ind, True, True), "ct", 1)
-        n_m = fin(g.tensor.matmul(T.PM[:, 0:256], T.M2[:], ind, True, True), "ct", 1)
-        codh = T["cod%d" % h]
-        cod = tt(codh[:], T.cI[:, cs], T.pre[:, cs], A.add, dep=[c, e_p])
-        xs = [act(T.X[:, E * (2 * h + i):E * (2 * h + i + 1)], codh[:, 0:64].indirect(T.rep[:, 32 * i:32 * i + 32]),
-                  dep=[cod, c_r]) for i in range(2)]
-        return n_c, n_m, xs
+            ts("ind%d" % i + x, ind[:, n * i:n * (i + 1)], T.qI[:, ls], float(i), None, A.is_equal, dep=["q" + x])
+        inds = seq("ind%d" + x, range(4))
+        mm("pc" + x, [(T.PC[:, 0:4 * n], T.NEG[:], ind[:], True, True)], inds + ["NEG"] + (["scn%d" % (b - 1)] if b else []))
+        mm("pm" + x, [(T.PM[:, 0:4 * n], T.M2[:], ind[:], True, True)], inds + ["M2"] + (["pos%d" % (b - 1)] if b else []))
+        op("scn" + x, "v", lambda scn=scn, n=n, x=x: V.tensor_tensor_scan(scn[:], T["d" + x][:], T.PC[:, 0:4 * n], 1.0e4,
+                                                                         A.min, A.subtract), ["pc" + x, "i_d" + x])
+        tt("pos" + x, pos[:], scn[:], T.PM[:, 0:4 * n], A.add, ["scn" + x, "pm" + x])
+        tt("ma" + x, ma[:], pos[:, 0:2 * n], pos[:, 2 * n:4 * n], A.max, ["pos" + x])
+        tt("mb" + x, mb[:], ma[:, 0:n], ma[:, n:2 * n], A.max, ["ma" + x])
+        ts("slot" + x, T.slot[:, ls], mb[:], -BIG, None, A.add, dep=["mb" + x])
+        for k in ks:
+            counted[k] = "slot" + x
+            tt("put%d" % k, T.W[:, WK * k:WK * k + NL].indirect(T.slot[:, 32 * k:32 * k + 32]), T.G[:, E * k:E * (k + 1)],
+               T.Y[:, E * k:E * (k + 1)], A.add, ["slot" + x, "G%d" % k, "Y%d" % k]
+               + (["cpW3"] if k else seq("E0%d", range(4))))
+    eng = engines(r, [[1, 2, 3]])
 
-    def slots(h, n_c, n_m):
-        c0 = 256 * h
-        wait("v", n_c, i_d)
-        a = fin(g.vector.tensor_tensor_scan(T.scn[:, c0:c0 + 256], T.d0[:], T.PC[:, 0:256], 1.0e4, A.min, A.add), "cv", 1)
-        p = tt(T.pos[:, c0:c0 + 256], T.scn[:, c0:c0 + 256], T.PM[:, 0:256], A.add, dep=[a, n_m])
-        a = tt(T.m1[:, 128 * h:128 * h + 128], T.pos[:, c0:c0 + 128], T.pos[:, c0 + 128:c0 + 256], A.max, dep=[p])
-        a = tt(T.m2[:, 64 * h:64 * h + 64], T.m1[:, 128 * h:128 * h + 64], T.m1[:, 128 * h + 64:128 * h + 128], A.max, dep=[a])
-        return ts(T.slot[:, 64 * h:64 * h + 64], T.m2[:, 64 * h:64 * h + 64], -BIG, None, A.add, dep=[a]), p
+    def ev(k, c0, n=CAP):
+        return T.W[:, WK * k + c0:WK * k + c0 + n]
 
-    PW = [T.PW0, T.PW1, T.PW2, T.PW3]
-    w_pe = [None] * P
-
-    def bucket(k, dep):
-        return tt(T.win[:, NL * k:NL * (k + 1)].indirect(T.slot[:, 32 * k:32 * k + 32]), T.X[:, E * k:E * (k + 1)],
-                  T.omask[:], A.mult, dep=dep + [z_win[k], c_om])
-
-    def wrap(k, a):
-        w_pe[k] = to_lists(PW[k][:, 0:40], T.win, NL * k, NL, [a])
-
-    where = {k: (b, i) for b, ks in enumerate(BATCH) for i, k in enumerate(ks)}
-    ed, ee = ev_dst(r), ev_eng(r)
-    own_ev = [None] * len(BATCH)
-
-    def out_lists(k):
-        b, i = where[k]
-        a = act(T["ev%d" % b][:, :, 10 * i:10 * i + 10], PW[k][:, 0:30], dep=[w_pe[k]])
-        own_ev[b] = act(T["land%d" % b][:, 3, 10 * i:10 * i + 10], PW[k][:, 30:40])
-        if k == BATCH[b][-1]:
-            n = 10 * len(BATCH[b])
-            remote([(ed[j], ee[ed[j]], [T["ev%d" % b][:, j, :]], T["land%d" % b][:, j, 0:n]) for j in range(3)],
-                   "ev%d" % b, [a])
-
-    s0 = shifts(0)
-    n_c, n_m, xa = classes(0, s0, None)
-    s1 = shifts(1)
-    empty(2)
-    empty(3)
-    z_V = act(T.V[:, 0:NL], T.ttab[:, 0:NL], scale=0.0)
-    sa, free = slots(0, n_c, n_m)
-    b0 = bucket(0, [sa, xa[0]])
-    n_c, n_m, xb = classes(1, s1, free)
-    wrap(0, b0)
-    out_lists(0)
-    wrap(1, bucket(1, [xa[1]]))
-    sb, _ = slots(1, n_c, n_m)
-    out_lists(1)
-    wrap(2, bucket(2, [sb, xb[0]]))
-    wrap(3, bucket(3, [xb[1]]))
-    out_lists(2)
-
-    def col(buf, k):
-        return buf[:, 40 * k:40 * k + 40]
+    for k in range(P):
+        remote("sendE%d" % k, [(cores[a], eng[cores[a]], [ev(k, CAP * bucket(r, a))],
+                               ev(k, CAP * (3 + senders(a).index(r)))) for a in others], "ev%d" % k, ["put%d" % k])
 
     def row(buf, k):
         return buf[:, NL * k:NL * (k + 1)]
 
-    def nb(k, j, n=None):
-        b, i = where[k]
-        buf, i = T["nb%d" % b], len(BATCH[b]) * j + i
-        return buf[:, i, :] if n is None else buf[:, i, 10 * n:10 * n + 10]
-
-    d_t, d_c, d_p, d_n = [None] * P, [None] * P, [None] * P, [None] * P
-
-    def decode(b):
-        ks = BATCH[b]
-        xb_, tb, cb = T["x%d" % b], T["t%d" % b], T["c%d" % b]
-        x = cp(xb_[:], T["land%d" % b][:, :, 0:10 * len(ks)], dep=[("ev%d" % b, n_ev), own_ev[b]])
-        a = ts(tb[:], xb_[:], 13, TT - 1, A.arith_shift_right, A.bitwise_and, dep=[x])
-        c = ts(cb[:], xb_[:], 8191, None, A.bitwise_and)
+    last = len(SRC) - 1
+    readers = ["u%d" % (last - last % 2), "u%d" % (last - (last + 1) % 2)]
+    batch = {}
+    for b, ks in enumerate(DEC):
+        x, kk, bank = str(b), slice(ks[0], ks[-1] + 1), PS[b % 2]
         for i, k in enumerate(ks):
-            cs = slice(10 * i, 10 * i + 10)
-            d_t[k] = cp(col(T.t16, k), tb[:, :, cs], dep=[a])
-            d_p[k] = ts(col(T.p16, k), xb_[:, :, cs], 0.0, None, A.is_lt)
-            d_c[k] = cp(col(T.cs16, k), cb[:, :, cs], dep=[c])
-        for n, (d, lim, op) in enumerate(((-1.0, NL, A.max), (1.0, WN - 1, A.min), (-128.0, NL, A.max),
-                                          (128.0, WN - 1, A.min))):
-            tk = ts(T["nb%d" % b][:, :, 10 * n:10 * n + 10], cb[:], d, float(lim), A.add, op)
-        for k in ks:
-            d_n[k] = tk
+            batch[k] = x
+            to_lists("pl%d" % k, bank[:, 40 * i:40 * i + 40], T.W, WK * k + 3 * CAP, NL,
+                     ["ev%d" % k, "put%d" % k, readers[b % 2]])
+        ts("x" + x, T.xI[:, kk, :], bank[:, 0:40 * len(ks)], -float(S * r), None, A.add, dep=seq("pl%d", ks))
+        readers[b % 2] = "x" + x
+        ts("c" + x, T.cI[:, kk, :], T.xI[:, kk, :], 4 * S - 1, None, A.bitwise_and, dep=["x" + x])
+        cp("c16" + x, T.c16[:, kk, :], T.cI[:, kk, :], ["c" + x])
+        for n, (d, lim, o) in enumerate(((-1.0, 0, A.max), (1.0, S - 1, A.min), (-128.0, 0, A.max), (128.0, S - 1, A.min))):
+            ts("nb%d" % n + x, T.nb[:, kk, 40 * n:40 * n + 40], T.cI[:, kk, :], d, float(lim), A.add, o, dep=["c" + x])
 
-    tA, tW, tL, tE, tV, tS = ([None] * P for _ in range(6))
+    def ag(k, n, p0, p1=None):
+        c0 = 3 * CAP + NL * n
+        return T["an%d" % k][:, c0 + CAP * p0:c0 + CAP * (p0 + 1 if p1 is None else p1)]
 
-    def times(k):
-        tA[k] = act(row(T.At, k), T.ttab[:, 0:TT].indirect(col(T.t16, k)), bias=float(TT * k), dep=[d_t[k], i_t1])
+    halves = ((0, 512), (512, NL))
+    used = ["scn%d" % last, "pos%d" % last]
+    nbV, nbS = [[] for _ in range(P)], [[] for _ in range(P)]
+    for k in range(P):
+        x, c16, before = str(k), T.c16[:, k, :], str(k - 1)
+        fk, here = WK * k + 3 * CAP, ["ev" + x, "put" + x]
+        mm("dA" + x, [(T.PA[:, a:b], T.Dsel[:], T.W[:, fk + a:fk + b], True, False) for a, b in halves],
+           here + ["Dsel"] + (["ex" + before] if k else ["Y0", "Y1"]))
+        mm("w" + x, [(T.PB[:, a:b], T.Wsel[:], T.W[:, fk + a:fk + b], True, True) for a, b in halves],
+           here + ["Wsel"] + (["W2" + before] if k else ["Y2", "Y3"]))
+        act("W2" + x, row(T.W2, k), T.PB[:, 0:NL], ["w" + x], F.Sign, scale=-1.0, bias=0.5)
+        act("gl" + x, row(T.Lg, k), T.L[:, 0:WN].indirect(c16), ["c16" + batch[k], "pL" + before if k else "r_lL"], scale=-1.0)
+        mm("dL" + x, [(T.PA[:, a:b], T.Dsel[:], T.Lg[:, NL * k + a:NL * k + b], False, True) for a, b in halves],
+           ["gl" + x, "dA" + x])
+        act("ex" + x, row(T.Ex, k), T.PA[:, 0:NL], ["dL" + x, "l_rate"], F.Exp, scale=T.ratec[:, 0:1])
+        if k < P - 1:
+            cp("pL" + x, T.L[:, 0:WN].indirect(c16), T.W[:, fk:fk + NL], ["gl" + x])
+        tt("gs" + x, row(T.tmp, k), T.V[:, 0:WN].indirect(c16), row(T.Ex, k), A.mult,
+           ["ex" + x] + (["ps" + before] if k else ["l_v1", "z_V"]))
+        tt("ps" + x, T.V[:, 0:WN].indirect(c16), row(T.tmp, k), row(T.W2, k), A.add,
+           ["gs" + x, "W2" + x] + (nbV[k - 1] + nbS[k - 1] if k else []))
+        ready = {p: [] for p in range(4)}
+        fused = [p for p0, p1, how in NBR[k] if how != "s" for p in range(p0, p1)]
 
-    def pols(k):
-        tW[k] = act(row(T.Wt, k), T.wtab[:, 0:8].indirect(col(T.p16, k)), dep=[d_p[k], z_w])
+        def neighbours(n, p0, p1, how):
+            name, dep = "n%d%d%d" % (k, p0, n), ["ps" + x, "nb%d" % n + batch[k]]
+            src = T.V[:, 0:WN].indirect(T.nb[:, k, 40 * n + 10 * p0:40 * n + 10 * p1])
+            if how == "s" or (how, n) == ("h", 0):
+                act(name, ag(k, n, p0, p1), src, dep)
+            elif n == 0:
+                cp(name, ag(k, 0, p0, p1), src, dep)
+            else:
+                tt(name, ag(k, 0, p0, p1), src, ag(k, 0, p0, p1), A.add, dep + ["n%d%d%d" % (k, p0, n - 1)])
+            (nbV if ops[name][0] == "v" else nbS)[k].append(name)
+            for p in range(p0, p1):
+                ready[p].append(name)
 
-    last_sL = [None]
+        for p0, p1, how in NBR[k]:
+            for n in range(4):
+                neighbours(n, p0, p1, how)
+        eng = engines(r, SENDS[k])
+        for i, ps in enumerate(SENDS[k]):
+            items = []
+            for p in ps:
+                a = senders(r)[p]
+                items.append((cores[a], eng[cores[a]], [ag(k, n, p) for n in range(1 if p in fused else 4)],
+                              T["an" + x][:, CAP * bucket(a, r):CAP * (bucket(a, r) + 1)]))
+            remote("sendA%d%d" % (k, i), items, "an" + x, [d for p in ps for d in ready[p]])
+        own = ready[0]
+        if 0 not in fused:
+            bank = [T.PC, T.PM][k % 2]
+            mm("oa" + x, [(bank[:, 0:CAP], T.Id[:], ag(k, n, 0), n == 0, n == 3) for n in range(4)],
+               own + ["Id", used[k % 2]])
+            act("oc" + x, ag(k, 0, 0), bank[:, 0:CAP], ["oa" + x])
+            own = ["oc" + x]
+            used[k % 2] = "oc" + x
+        for q, c0, c1 in PICK[k]:
+            out = T.yst[:, E * k + 16 * c0:E * k + 16 * c1]
+            src = T["an" + x][:, 0:NL].indirect(T.slot[:, 32 * k + c0:32 * k + c1])
+            (cp if q == "v" else act)("pick" + q + x, out, src, ["an" + x, counted[k]] + own)
+            dma("st" + q + x, "s" if (q, k) == ("s", P - 1) else "y", T.y[:, E * k + 16 * c0:E * k + 16 * c1], out, "st",
+                ["pick" + q + x])
 
-    def get_last(k):
-        tL[k] = tt(row(T.dt, k), T.L[:, 0:WN].indirect(col(T.cs16, k)), row(T.At, k), A.subtract,
-                   dep=[d_c[k], tA[k], l_L, z_L, last_sL[0]])
+    def cls(x):
+        return ["u" + x, "q" + x] + seq("ind%d" + x, range(4))
 
-    def put_last(k):
-        last_sL[0] = cp(T.L[:, 0:WN].indirect(col(T.cs16, k)), row(T.At, k), dep=[tL[k]])
+    def slots(x):
+        return [y + x for y in ("scn", "pos", "ma", "mb", "slot")]
 
-    def decay(k):
-        tE[k] = act(row(T.Ex, k), row(T.dt, k), F.Exp, scale=T.ratec[:, 0:1], dep=[tL[k], l_rate])
+    def dec(x):
+        return ["x" + x, "c" + x, "c16" + x]
 
-    def get_state(k):
-        tV[k] = tt(row(T.tmp, k), T.V[:, 0:WN].indirect(col(T.cs16, k)), row(T.Ex, k), A.mult,
-                   dep=[tE[k], l_v, z_V, tS[k - 1] if k else None])
+    def nbs(x):
+        return seq("nb%d" + x, range(4))
 
-    def put_state(k, readers):
-        tS[k] = tt(T.V[:, 0:WN].indirect(col(T.cs16, k)), row(T.tmp, k), row(T.Wt, k), A.add,
-                   dep=[tV[k], tW[k]] + readers)
+    order = {
+        "y": ["l_s0", "r_tL", "l_s1", "r_tH", "r_s0H", "r_s0L", "l_last", "l_rate", "l_v0", "r_s1H", "r_s1L", "cpW2", "cpW3",
+              "l_v1", "r_lH", "r_lL", "sts0", "sts1", "sts2", "stv3"],
+        "g": ["i_p", "i_cnt", "i_e", "i_blk", "i_k"] + seq("Sm%d", range(SM_G, 16)) + ["M1", "M2", "i_d0", "i_d1", "z_Lg"]
+        + ["sendE0", "i_d2", "sendE1", "z_V", "sendE2", "sendE3"] + [n for n in ops if n[:5] == "sendA"],
+        "t": ["y00", "y01", "sh0", "pc0", "pm0", "sh1", "y10", "y11", "y20", "pc1", "pm1", "sh2", "y21", "pc2", "pm2", "y30", "y31",
+              "pl0", "dA0", "w0", "pl1", "dL0", "w1", "dA1", "pl2", "dL1", "w2", "pl3", "dA2", "dL2", "w3", "dA3", "dL3"]
+        + [n for n in ops if n[:2] == "oa"],
+        "v": ["z_B", "oI", "pf", "of", "gf", "m16", "Bf", "eb", "mT", "mU", "s0H", "s0L", "NEG", "zp", "t128", "zI", "gn", "zH",
+              "gm", "zL", "gb", "t16"] + seq("Sm%d", range(SM_S, SM_G)) + ["s1H", "s1L", "pixr", "lastH", "lastL"]
+        + cls("0") + slots("0") + ["put0"] + cls("1") + slots("1") + cls("2") + ["put1"] + slots("2") + ["put2"] + dec("0")
+        + ["put3", "x1", "nb00", "c1", "nb10", "c161", "pL0", "nb20", "gs0", "nb30", "ps0"] + dec("2") + ["pL1"] + nbV[0]
+        + dec("3") + nbs("1") + ["gs1", "ps1", "pL2", "Id"] + nbV[1] + nbs("2") + ["gs2"] + nbs("3") + ["ps2"] + nbV[2]
+        + ["gs3", "ps3"] + nbV[3] + ["pickv3"],
+        "s": ["l_tm", "l_pol", "l_pix", "tH"] + seq("Sm%d", range(SM_S)) + ["Bm"] + seq("E0%d", range(4)) + ["G0", "G1"]
+        + seq("E1%d", range(4)) + ["Y0", "G2", "G3", "Y1", "z_Ls", "Y2", "Dsel", "Wsel", "Y3"]
+        + ["gl0", "W20", "ex0", "gl1", "W21", "ex1"] + nbS[0] + ["gl2", "W22", "ex2"] + nbS[1] + ["gl3", "W23", "ex3"]
+        + nbS[2] + ["oc0", "oc1", "picks0"] + nbS[3] + ["oc2", "picks1", "picks2", "oc3", "picks3", "sts3"],
+    }
 
-    ANS = [T.ans0, T.ans1, T.ans2, T.ans3]
-
-    def ag(k, j, n=None):
-        c0 = NL * (3 * k + j)
-        return T.ag[:, c0:c0 + NL] if n is None else T.ag[:, c0 + CAP * n:c0 + CAP * (n + 1)]
-
-    def four(k, j):
-        out = ANS[k][:, 3 * CAP:3 * CAP + NL] if j == 3 else ag(k, j)
-        return act(out, T.V[:, 0:WN].indirect(nb(k, j)), dep=[tS[k], d_n[k]])
-
-    def summed(k, js, begun):
-        tk = dict(begun)
-        nxt = {j: 1 if j in begun else 0 for j in js}
-        while any(nxt[j] < 4 for j in js):
-            for j in js:
-                n = nxt[j]
-                if n < 4:
-                    src = T.V[:, 0:WN].indirect(nb(k, j, n))
-                    if n == 0:
-                        tk[j] = cp(ag(k, j, 0), src, dep=[tS[k], d_n[k]])
-                    else:
-                        tk[j] = tt(ag(k, j, 0), src, ag(k, j, 0), A.add, dep=[tS[k], tk[j]])
-                    nxt[j] = n + 1
-        return [tk[j] for j in js]
-
-    ad, ae = an_dst(r), an_eng(r)
-    far = [j for j in range(3) if topo.chip(ad[j]) != topo.chip(core)]
-    near = [j for j in range(3) if j not in far]
-
-    def send(k, dep, sums=()):
-        remote([(ad[j], ae[ad[j]], [ag(k, j, 0)] if j in sums else [ag(k, j, n) for n in range(4)],
-                 ANS[k][:, CAP * j:CAP * (j + 1)]) for j in range(3)], "an%d" % k, dep)
-
-    def own_dma(k, dep):
-        a = dma("g", ANS[k][:, 480:800], ANS[k][:, 800:1120], "accA", dep=dep, accum_op=A.add)
-        return dma("g", ANS[k][:, 480:640], ANS[k][:, 640:800], "accB%d" % k, dep=[a], accum_op=A.add)
-
-    def pick(q, k, c0, c1, dep):
-        out = T.yst[:, E * k + 16 * c0:E * k + 16 * c1]
-        src = ANS[k][:, 0:NL].indirect(T.slot[:, 32 * k + c0:32 * k + c1])
-        return cp(out, src, dep=dep) if q == "v" else act(out, src, dep=dep + [sb])
-
-    def store(q, c0, c1, dep):
-        return dma(q, T.y[:, c0:c1], T.yst[:, c0:c1], "st", dep=dep)
-
-    decode(0)
-    times(0)
-    out_lists(3)
-    pols(0)
-    get_last(0)
-    decay(0)
-    put_last(0)
-    decode(1)
-    get_state(0)
-    put_state(0, [])
-    times(1)
-    pols(1)
-    own = [None] * P
-    for k in (0, 1):
-        get_last(k + 1)
-        four(k, 0)
-        decay(k + 1)
-        put_last(k + 1)
-        if k == 0:
-            decode(2)
-        get_state(k + 1)
-        four(k, 1)
-        a = four(k, 2)
-        send(k, [a])
-        a = four(k, 3)
-        own[k] = own_dma(k, [a])
-        put_state(k + 1, [a])
-        times(k + 2)
-        pols(k + 2)
-    get_last(3)
-    nr = [four(2, j) for j in near]
-    decay(3)
-    o2 = four(2, 3)
-    sm = summed(2, far, {})
-    get_state(3)
-    send(2, sm + nr, far)
-    put_state(3, [o2] + sm)
-    store("y", 0, E, [pick("s", 0, 0, 32, [("an0", n_an), own[0]])])
-
-    begun = {j: act(ag(3, j, 0), T.V[:, 0:WN].indirect(nb(3, j, 0)), dep=[tS[3], d_n[3]]) for j in far[1:]}
-    nr = [four(3, j) for j in near]
-    o3 = four(3, 3)
-    sm = summed(3, far, begun)
-    send(3, sm + nr, far)
-    half = [tt(ANS[k][:, 480:800], ANS[k][:, 480:800], ANS[k][:, 800:1120], A.add, dep=[o]) for k, o in ((2, o2), (3, o3))]
-    for k in (2, 3):
-        own[k] = tt(ANS[k][:, 480:640], ANS[k][:, 480:640], ANS[k][:, 640:800], A.add, dep=[half[k - 2]])
-    for k in (1, 2):
-        store("y", E * k, E * (k + 1), [pick("s", k, 0, 32, [("an%d" % k, n_an), own[k]])])
-    ya = pick("v", 3, 0, 16, [("an3", n_an), own[3]])
-    yb = pick("s", 3, 16, 32, [("an3", n_an), own[3]])
-    store("y", E * 3, E * 3 + 256, [ya])
-    a = store("s", E * 3 + 256, E * 4, [yb])
-    wait("y", a)
-    for s, n in cnt.items():
-        if max(waited[q].get(s, 0) for q in Q) < n:
-            wait("g", (s, n))
+    token, total = {s: (s, n) for s, n in arrive.items()}, {}
+    for q, names in order.items():
+        for name in names:
+            sem = ops[name][3] or "c" + q
+            total[sem] = total.get(sem, 0) + (16 if ops[name][3] else 1)
+            token[name] = (sem, total[sem])
+    for name, (q, fn, dep, sem) in ops.items():
+        if sem:
+            token[name] = (sem, total[sem])
+    top = {}
+    for q, names in order.items():
+        seen = {}
+        for name in names:
+            _, fn, dep, sem = ops[name]
+            for s, n in sorted((token[d] for d in dep), reverse=True):
+                if (q, s) != ("t", "ct") and seen.get(s, 0) < n:
+                    Q[q].wait_ge(T.sem[s], n)
+                    seen[s] = n
+                    top[s] = max(top.get(s, 0), n)
+            ins = fn()
+            if sem != "remote":
+                ins.then_inc(T.sem[sem or "c" + q], 16 if sem else 1)
+    total["sent"] = sent[0]
+    for s, n in total.items():
+        if s != "remote" and top.get(s, 0) < n:
+            g.wait_ge(T.sem[s], n)

@@ -9,11 +9,16 @@ WK = 7 * CAP
 AK = 3 * CAP + 4 * NL
 BIG = 1025.0
 T_HI, T_LO, PIX_HI, PIX_LO = 2, 6, 7, 9
-SRC = [[0], [1], [2, 3]]
-DEC = [[0], [1], [2], [3]]
-L_S = TT + 1024
-SM_S, SM_G = 11, 11
+SW = 134
 BF = "bfloat16"
+
+SRC = [[0], [1], [2, 3]]
+DEC = [[0], [1], [2, 3]]
+SM_S, SM_G = 9, 9
+NBR = [[(0, 4, "s")], [(0, 4, "s")], [(2, 4, "v"), (0, 2, "s")], [(2, 3, "h"), (3, 4, "h"), (1, 2, "h"), (0, 1, "s")]]
+SENDS = [[[1, 2, 3]]] * 3 + [[[2], [3, 1]]]
+EV_MOST = [4, 4, 8, 8]
+PICK = [[("s", 0, 32)], [("v", 0, 32)], [("s", 0, 32)]] + [[("v", 0, 16), ("s", 16, 32)]]
 
 
 def _sb(cols, dt="float32"):
@@ -24,16 +29,15 @@ SCRATCH = {
     "tmI": _sb(128, "int32"), "pixI": _sb(128, "int32"), "polI": _sb(128, "int32"),
     "lastI": _sb(256, "int32"), "ratec": _sb(4), "s0I": _sb(256, "int32"), "s1I": _sb(256, "int32"),
     "lastH": _sb(256, BF), "lastL": _sb(256, BF),
-    "zp": _sb(128), "zI": _sb(128), "zH": _sb(128, BF), "zL": _sb(128, BF), "pixr": _sb(128), "t16": _sb(128, "uint16"),
+    "zH": _sb(128, BF), "zL": _sb(128, BF), "t16": _sb(128, "uint16"),
     "pI": _sb(4, "int32"), "oI": _sb(4, "int32"), "col": _sb(8), "m16": _sb(16), "gm": _sb(4), "gn": _sb(4),
-    "gb": _sb(4), "eb": _sb(4), "io8": _sb(8), "cnt": _sb(CAP, BF), "blk": _sb(128, BF), "tH": _sb(128, BF),
-    "Bf": _sb(144, BF), "Bm": _sb(144, BF), "NEG": _sb(128, BF), "M1": _sb(128, BF), "M2": _sb(128, BF),
-    "Dsel": _sb(128, BF), "Wsel": _sb(128, BF), "Sm": _sb([16, 130], BF),
-    "G": _sb(P * E, BF), "Y": _sb(P * E, BF), "Id": _sb(128),
-    "W": _sb(P * WK, BF),
+    "gb": _sb(4), "eb": _sb(4), "io8": _sb(8), "cnt": _sb(CAP, BF),
+    "Bm": _sb(144, BF), "NEG": _sb(128, BF), "M2": _sb(128, BF),
+    "Dsel": _sb(128, BF), "Wsel": _sb(128, BF), "Sm": _sb(9 * SW, BF),
+    "G": _sb(P * E, BF), "Y": _sb(P * E, BF), "Id": _sb(128), "W": _sb(P * WK, BF),
     "uI": _sb(128, "int32"), "qI": _sb(128, "int32"), "slot": _sb(128, "uint16"),
     "xI": _sb([P, 40], "int32"), "cI": _sb([P, 40], "int32"), "c16": _sb([P, 40], "uint16"), "nb": _sb([P, 160], "uint16"),
-    "V": _sb(WN), "L": _sb(WN, BF), "Lg": _sb(P * NL, BF), "Ex": _sb(P * NL), "W2": _sb(P * NL), "tmp": _sb(P * NL),
+    "V": _sb(WN), "L": _sb(S + 7 * SW, BF), "Lg": _sb(P * NL, BF), "Ex": _sb(P * NL), "W2": _sb(P * NL), "tmp": _sb(P * NL),
     "yst": _sb(P * E),
     "PA": ("psum", [128, 1024], "float32"), "PB": ("psum", [128, 1024], "float32"),
 }
@@ -41,16 +45,12 @@ for _k in range(P):
     SCRATCH["an%d" % _k] = _sb(AK)
 for _b, _ks in enumerate(SRC):
     _n = 32 * len(_ks)
-    SCRATCH.update({"d%d" % _b: _sb(4 * _n), "ind%d" % _b: _sb(4 * _n, BF), "scn%d" % _b: _sb(4 * _n),
+    SCRATCH.update({"ind%d" % _b: _sb(4 * _n, BF), "scn%d" % _b: _sb(4 * _n),
                     "pos%d" % _b: _sb(4 * _n), "ma%d" % _b: _sb(2 * _n), "mb%d" % _b: _sb(_n)})
 for _x in ("PS0", "PS1", "PC", "PM"):
     SCRATCH[_x] = ("psum", [128, 512], "float32")
-SEMAPHORES = ["cv", "cs", "ct", "cg", "ltm", "lsh", "lpix", "lpol", "llast", "lv", "lrate", "rowB", "rowC", "rowL", "cpW", "ls0",
+SEMAPHORES = ["cv", "cs", "ct", "cg", "ltm", "ls0", "ls1", "lpix", "lpol", "llast", "lv", "lrate", "rowB", "rowC", "rowL", "cpW",
               "sent", "st"] + ["%s%d" % (_x, _k) for _x in ("ev", "an") for _k in range(P)]
-
-NBR = [[(0, 4, "s")], [(0, 4, "s")], [(2, 4, "v"), (0, 2, "s")], [(2, 3, "v"), (3, 4, "v"), (1, 2, "s"), (0, 1, "s")]]
-SENDS = [[[1, 2, 3]]] * 3 + [[[1, 2], [3]]]
-PICK = [[("s", 0, 32)]] * 3 + [[("v", 0, 16), ("s", 16, 32)]]
 
 
 def seq(pat, xs):
@@ -64,11 +64,11 @@ def _bits(es):
     return m
 
 
-def _share(topo, src, dsts, near_most):
+def _share(topo, src, dsts, most):
     far = [d for d in dsts if topo.chip(d) != topo.chip(src)]
     near = [d for d in dsts if topo.chip(d) == topo.chip(src)]
     out, used = {}, []
-    for grp, most in ((far, 16), (near, near_most)):
+    for grp in (far, near):
         for i, d in enumerate(grp):
             free = [e for e in topo.engines(src, d) if e not in used]
             n = min(len(free) // (len(grp) - i), most)
@@ -141,20 +141,20 @@ def rank_program(g, core, T, topo):
     def bucket(src, a):
         return 3 - (a - src) % N
 
-    def engines(a, calls):
+    def engines(a, calls, most=8):
         out = {}
         for ps in calls:
-            out.update(_share(topo, cores[a], [cores[senders(a)[p]] for p in ps], 8))
+            out.update(_share(topo, cores[a], [cores[senders(a)[p]] for p in ps], most))
         return out
 
     others = senders(r)[1:]
     arrive = {}
     for k in range(P):
-        arrive["ev%d" % k] = sum(len(engines(a, [[1, 2, 3]])[core]) for a in others)
+        arrive["ev%d" % k] = sum(len(engines(a, [[1, 2, 3]], EV_MOST[k])[core]) for a in others)
         arrive["an%d" % k] = sum(len(engines(a, SENDS[k])[core]) for a in others)
 
     dma("l_s0", "y", T.s0I[:], T.sh[:, 0:2 * TT], "ls0")
-    dma("l_s1", "y", T.s1I[:], T.sh[:, 2 * TT:4 * TT], "lsh")
+    dma("l_s1", "y", T.s1I[:], T.sh[:, 2 * TT:4 * TT], "ls1")
     dma("l_tm", "s", T.tmI[:], T.tm[:], "ltm")
     dma("l_pix", "s", T.pixI[:], T.pix[:], "lpix")
     dma("l_pol", "s", T.polI[:], T.pol[:], "lpol")
@@ -163,18 +163,32 @@ def rank_program(g, core, T, topo):
         dma("l_v%d" % h, "y", T.V[:, S // 2 * h:S // 2 * (h + 1)], T.v[:, S // 2 * h:S // 2 * (h + 1)], "lv")
     dma("l_rate", "y", T.ratec[:, 0:1], T.rate[:], "lrate")
 
+    def carve(buf, c0, **sizes):
+        out = {}
+        for name, n in sizes.items():
+            out[name] = buf[:, c0:c0 + n]
+            out[name + "0"] = c0
+            c0 += n
+        return out, c0
+
+    U, end = carve(T.L, TT, s0H=256, s0L=256, s1H=256, s1L=256, tH=128, blk=128, M1=128, Bf=144)
+    U.update(carve(T.V, S + CAP, d1=128, d2=256, pixr=128, zp=128, zI=128)[0])
+
+    def Sm(j, c0=0, n=SW):
+        buf, c = (T.L, S + SW * j) if j < 7 else (T.Sm, SW * (j - 7))
+        return buf[:, c + c0:c + c0 + n]
+
     pf, of, gf, mT, mU, t128 = (T.col[:, i:i + 1] for i in range(6))
     op("i_p", "g", lambda: g.iota(T.pI[:, 0:1], [[0, 1]], 0, 1))
     iota("i_cnt", T.cnt[:], [[1, CAP]])
-    iota("i_blk", T.blk[:], [[16, 8], [0, 16]])
+    iota("i_blk", U["blk"], [[16, 8], [0, 16]])
     iota("i_k", T.io8[:, 0:4], [[TT, 4]])
     iota("i_e", T.io8[:, 4:8], [[256 - S, 4]], S * (r + 4))
-    for b, ks in enumerate(SRC):
-        iota("i_d%d" % b, T["d%d" % b][:], [[-CAP, 4], [0, len(ks)], [1000, 32]], 3 * CAP)
-    iota("z_V", T.V[:, S:WN], [[0, WN - S]])
-    iota("z_Lg", T.L[:, L_S + CAP:WN], [[0, WN - L_S - CAP]])
+    for n in (1, 2):
+        iota("i_d%d" % n, U["d%d" % n], [[-CAP, 4], [0, n], [1000, 32]], 3 * CAP)
+    iota("z_Lg", T.L[:, end:S], [[0, S - end]])
     op("z_B", "v", lambda: V.memset(T.L[:, 0:TT], 0.0))
-    act("z_Ls", T.L[:, L_S:L_S + CAP], T.cnt[:], ["i_cnt"], F.Exp, scale=0.0)
+    act("z_Vs", T.V[:, S:S + CAP], T.cnt[:], ["i_cnt"], F.Exp, scale=0.0)
     ts("oI", T.oI[:, 0:1], T.pI[:, 0:1], 15, None, A.bitwise_and, dep=["i_p"])
     cp("pf", pf, T.pI[:, 0:1], ["i_p"])
     cp("of", of, T.oI[:, 0:1], ["oI"])
@@ -184,7 +198,7 @@ def rank_program(g, core, T, topo):
     def m(o):
         return T.m16[:, o:o + 1]
 
-    ts("Bf", T.Bf[:], T.cnt[:, 0:144], -15.0, gf, A.add, A.is_equal, dep=["gf", "i_cnt"])
+    ts("Bf", U["Bf"], T.cnt[:, 0:144], -15.0, gf, A.add, A.is_equal, dep=["gf", "i_cnt"])
     ts("eb", T.eb[:], T.io8[:, 4:8], m(PIX_HI), None, A.mult, dep=["m16", "i_e"])
     tt("mT", mT, m(T_HI), m(T_LO), A.add, ["m16"])
     ts("mU", mU, mT, 0.0, None, A.is_equal, dep=["mT"])
@@ -192,47 +206,45 @@ def rank_program(g, core, T, topo):
     tt("gn", T.gn[:], T.m16[:, 0:16:4], T.m16[:, 1:16:4], A.add, ["m16"])
     ts("gm", T.gm[:], T.gn[:], t128, None, A.add, dep=["gn", "t128"])
     ts("gb", T.gb[:], T.io8[:, 0:4], m(T_HI), None, A.mult, dep=["m16", "i_k"])
-    ts("NEG", T.NEG[:], T.blk[:], gf, -1.0, A.is_equal, A.mult, dep=["gf", "i_blk"])
+    ts("NEG", T.NEG[:], U["blk"], gf, -1.0, A.is_equal, A.mult, dep=["gf", "i_blk"])
     ts("Id", T.Id[:], T.cnt[:, 0:128], pf, None, A.is_equal, dep=["pf", "i_cnt"])
-    op("M1", "g", lambda: g.affine_select(T.M1[:], T.NEG[:], [[-1, 128]], A.is_gt, 0.0, 0, 1), ["NEG"])
-    op("M2", "g", lambda: g.affine_select(T.M2[:], T.M1[:], [[-1, 128]], A.not_equal, BIG - 1.0, 0, 1), ["M1"])
-    act("tH", T.tH[:], T.cnt[:, 0:128], ["of", "i_cnt"], scale=0.0, bias=of)
-    act("Bm", T.Bm[:], T.Bf[:], ["Bf", "mU"], scale=mU)
+    op("M1", "g", lambda: g.affine_select(U["M1"], T.NEG[:], [[-1, 128]], A.is_gt, 0.0, 0, 1), ["NEG"])
+    op("M2", "g", lambda: g.affine_select(T.M2[:], U["M1"], [[-1, 128]], A.not_equal, BIG - 1.0, 0, 1), ["M1"])
+    act("tH", U["tH"], T.cnt[:, 0:128], ["of", "i_cnt"], scale=0.0, bias=of)
+    act("Bm", T.Bm[:], U["Bf"], ["Bf", "mU"], scale=mU)
     act("Dsel", T.Dsel[:], T.NEG[:], ["NEG", "mT"], scale=mT)
     act("Wsel", T.Wsel[:], T.NEG[:], ["NEG", "m16"], scale=m(PIX_HI))
+    src = T.L[:, U["Bf0"] + 15 - PIX_LO:U["Bf0"] + 15 - PIX_LO + SW]
     for j in range(16):
-        src = T.Bf[:, 15 - PIX_LO:145 - PIX_LO]
         if j >= SM_G:
-            op("Sm%d" % j, "g", lambda j=j, src=src: g.affine_select(T.Sm[:, j, :], src, [[1, 130]], A.is_equal, 0.0,
-                                                                     j - PIX_LO, -1), ["Bf"])
+            op("Sm%d" % j, "g", lambda j=j, src=src: g.affine_select(Sm(j), src, [[1, SW]], A.is_equal, 0.0, j - PIX_LO, -1),
+               ["Bf"])
         elif j < SM_S:
-            act("Sm%d" % j, T.Sm[:, j, :], src, ["Bf", "m16"], scale=m(j))
+            act("Sm%d" % j, Sm(j), src, ["Bf", "m16"], scale=m(j))
         else:
-            ts("Sm%d" % j, T.Sm[:, j, :], src, m(j), None, A.mult, dep=["Bf", "m16"])
-    for k in range(2):
-        for j in range(4):
-            act("E%d%d" % (k, j), T.W[:, WK * k + CAP * j:WK * k + CAP * (j + 1)], T.cnt[:], ["eb", "i_cnt"],
-                scale=m(PIX_LO), bias=T.eb[:, j:j + 1])
-    for k in range(2, P):
-        dma("cpW%d" % k, "y", T.W[:, WK * k:WK * k + NL], T.W[:, WK:WK + NL], "cpW", seq("E1%d", range(4)))
+            ts("Sm%d" % j, Sm(j), src, m(j), None, A.mult, dep=["Bf", "m16"])
+    for j in range(4):
+        act("E%d" % j, T.W[:, CAP * j:CAP * (j + 1)], T.cnt[:], ["eb", "i_cnt"], scale=m(PIX_LO), bias=T.eb[:, j:j + 1])
+    for k in range(1, P):
+        dma("cpW%d" % k, "y", T.W[:, WK * k:WK * k + NL], T.W[:, 0:NL], "cpW", seq("E%d", range(4)))
 
-    part = {x + y: T.L[:, TT + 256 * i:TT + 256 * (i + 1)] for i, (x, y) in enumerate(("0H", "0L", "1H", "1L"))}
-    ts("zp", T.zp[:], T.polI[:], 16384.0, -16384.0, A.mult, A.add, dep=["l_pol"])
-    tt("zI", T.zI[:], T.pixI[:], T.zp[:], A.add, ["zp", "l_pix"])
+    ts("zp", U["zp"], T.polI[:], 16384.0, -16384.0, A.mult, A.add, dep=["l_pol"])
+    tt("zI", U["zI"], T.pixI[:], U["zp"], A.add, ["zp", "l_pix"])
     for x, ld in (("s0", "l_s0"), ("s1", "l_s1"), ("last", "l_last"), ("z", "zI")):
-        hi, lo = (part[x[1] + "H"], part[x[1] + "L"]) if x[0] == "s" else (T[x + "H"][:], T[x + "L"][:])
-        cp(x + "H", hi, T[x + "I"][:], [ld])
-        tt(x + "L", lo, T[x + "I"][:], hi, A.subtract, [x + "H"])
+        whole, hi, lo = (U[x + y] if x + y in U else T[x + y][:] for y in "IHL")
+        cp(x + "H", hi, whole, [ld])
+        tt(x + "L", lo, whole, hi, A.subtract, [x + "H"])
     cp("t16", T.t16[:], T.tmI[:], ["l_tm"])
-    ts("pixr", T.pixr[:], T.pixI[:], float(S * ((N - r) % N)), None, A.add, dep=["l_pix"])
-    dma("r_tH", "y", T.L[T_HI::16, 0:TT], T.tH[:], "rowB", ["z_B", "tH"])
+    ts("pixr", U["pixr"], T.pixI[:], float(S * ((N - r) % N)), None, A.add, dep=["l_pix"])
+    dma("r_tH", "y", T.L[T_HI::16, 0:TT], U["tH"], "rowB", ["z_B", "tH"])
     dma("r_tL", "y", T.L[T_LO::16, 0:TT], T.cnt[:, 0:128], "rowB", ["z_B", "i_cnt"])
-    dma("r_s0H", "y", T.L[0::8, 0:TT], part["0H"], "rowB", ["z_B", "s0H"])
-    dma("r_s0L", "y", T.L[1::8, 0:TT], part["0L"], "rowB", ["z_B", "s0L"])
-    dma("r_s1H", "y", T.L[4::8, 0:TT], part["1H"], "rowC", ["G0", "G1", "s1H"])
-    dma("r_s1L", "y", T.L[5::8, 0:TT], part["1L"], "rowC", ["G0", "G1", "s1L"])
-    dma("r_lH", "y", T.L[T_HI::16, 0:S], T.lastH[:], "rowL", ["z_Lg", "z_Ls", "lastH"] + seq("G%d", range(P)))
-    dma("r_lL", "y", T.L[T_LO::16, 0:S], T.lastL[:], "rowL", ["z_Lg", "z_Ls", "lastL"] + seq("G%d", range(P)))
+    dma("r_s0H", "y", T.L[0::8, 0:TT], U["s0H"], "rowB", ["z_B", "s0H"])
+    dma("r_s0L", "y", T.L[1::8, 0:TT], U["s0L"], "rowB", ["z_B", "s0L"])
+    dma("r_s1H", "y", T.L[4::8, 0:TT], U["s1H"], "rowC", ["G0", "G1", "s1H"])
+    dma("r_s1L", "y", T.L[5::8, 0:TT], U["s1L"], "rowC", ["G0", "G1", "s1L"])
+    done = ["z_Lg", "M2", "Bm"] + seq("G%d", range(P)) + seq("Sm%d", range(16))
+    dma("r_lH", "y", T.L[T_HI::16, 0:S], T.lastH[:], "rowL", done + ["lastH"])
+    dma("r_lL", "y", T.L[T_LO::16, 0:S], T.lastL[:], "rowL", done + ["lastL"])
 
     PY = [T.PA, T.PB]
     PS = [T.PS0, T.PS1]
@@ -242,8 +254,8 @@ def rank_program(g, core, T, topo):
             scale=T.gm[:, 2 * (k % 2) + k // 2:2 * (k % 2) + k // 2 + 1], bias=T.gb[:, k:k + 1])
         for h in range(2):
             js = range(8 * h, 8 * h + 8)
-            mm("y%d%d" % (k, h), [(PY[k // 2][:, c0 + j:c0 + E:16], T.Sm[:, j, PIX_LO - row:PIX_LO - row + 128], T[f][:, ls],
-                                   i == 0, i == 1) for j in js for i, (f, row) in enumerate((("zH", PIX_HI), ("zL", PIX_LO)))],
+            mm("y%d%d" % (k, h), [(PY[k // 2][:, c0 + j:c0 + E:16], Sm(j, PIX_LO - to, 128), T[f][:, ls], i == 0, i == 1)
+                                  for j in js for i, (f, to) in enumerate((("zH", PIX_HI), ("zL", PIX_LO)))],
                seq("Sm%d", js) + ["zH", "zL"])
         act("Y%d" % k, T.Y[:, es], PY[k // 2][:, c0:c0 + E], seq("y%d%%d" % k, range(2)))
     counted = {}
@@ -252,15 +264,15 @@ def rank_program(g, core, T, topo):
         ls = slice(32 * ks[0], 32 * ks[0] + n)
         ind, scn, pos, ma, mb = (T[y + x] for y in ("ind", "scn", "pos", "ma", "mb"))
         to_lists("sh" + x, PS[b % 2][:, 0:n], T.G, E * ks[0], 16 * n, seq("G%d", ks) + (["u%d" % (b - 2)] if b > 1 else []))
-        tt("u" + x, T.uI[:, ls], PS[b % 2][:, 0:n], T.pixr[:, ls], A.add, ["sh" + x, "pixr"])
+        tt("u" + x, T.uI[:, ls], PS[b % 2][:, 0:n], T.V[:, U["pixr0"] + ls.start:U["pixr0"] + ls.stop], A.add, ["sh" + x, "pixr"])
         ts("q" + x, T.qI[:, ls], T.uI[:, ls], 12, 3, A.arith_shift_right, A.bitwise_and, dep=["u" + x])
         for i in range(4):
             ts("ind%d" % i + x, ind[:, n * i:n * (i + 1)], T.qI[:, ls], float(i), None, A.is_equal, dep=["q" + x])
         inds = seq("ind%d" + x, range(4))
         mm("pc" + x, [(T.PC[:, 0:4 * n], T.NEG[:], ind[:], True, True)], inds + ["NEG"] + (["scn%d" % (b - 1)] if b else []))
         mm("pm" + x, [(T.PM[:, 0:4 * n], T.M2[:], ind[:], True, True)], inds + ["M2"] + (["pos%d" % (b - 1)] if b else []))
-        op("scn" + x, "v", lambda scn=scn, n=n, x=x: V.tensor_tensor_scan(scn[:], T["d" + x][:], T.PC[:, 0:4 * n], 1.0e4,
-                                                                         A.min, A.subtract), ["pc" + x, "i_d" + x])
+        op("scn" + x, "v", lambda scn=scn, n=n: V.tensor_tensor_scan(scn[:], U["d%d" % (n // 32)], T.PC[:, 0:4 * n], 1.0e4,
+                                                                    A.min, A.subtract), ["pc" + x, "i_d%d" % len(ks)])
         tt("pos" + x, pos[:], scn[:], T.PM[:, 0:4 * n], A.add, ["scn" + x, "pm" + x])
         tt("ma" + x, ma[:], pos[:, 0:2 * n], pos[:, 2 * n:4 * n], A.max, ["pos" + x])
         tt("mb" + x, mb[:], ma[:, 0:n], ma[:, n:2 * n], A.max, ["ma" + x])
@@ -268,14 +280,13 @@ def rank_program(g, core, T, topo):
         for k in ks:
             counted[k] = "slot" + x
             tt("put%d" % k, T.W[:, WK * k:WK * k + NL].indirect(T.slot[:, 32 * k:32 * k + 32]), T.G[:, E * k:E * (k + 1)],
-               T.Y[:, E * k:E * (k + 1)], A.add, ["slot" + x, "G%d" % k, "Y%d" % k]
-               + (["cpW3"] if k else seq("E0%d", range(4))))
-    eng = engines(r, [[1, 2, 3]])
+               T.Y[:, E * k:E * (k + 1)], A.add, ["slot" + x, "G%d" % k, "Y%d" % k, "cpW3"])
 
     def ev(k, c0, n=CAP):
         return T.W[:, WK * k + c0:WK * k + c0 + n]
 
     for k in range(P):
+        eng = engines(r, [[1, 2, 3]], EV_MOST[k])
         remote("sendE%d" % k, [(cores[a], eng[cores[a]], [ev(k, CAP * bucket(r, a))],
                                ev(k, CAP * (3 + senders(a).index(r)))) for a in others], "ev%d" % k, ["put%d" % k])
 
@@ -318,9 +329,9 @@ def rank_program(g, core, T, topo):
            ["gl" + x, "dA" + x])
         act("ex" + x, row(T.Ex, k), T.PA[:, 0:NL], ["dL" + x, "l_rate"], F.Exp, scale=T.ratec[:, 0:1])
         if k < P - 1:
-            cp("pL" + x, T.L[:, 0:WN].indirect(c16), T.W[:, fk:fk + NL], ["gl" + x])
+            cp("pL" + x, T.L[:, 0:WN].indirect(c16), T.W[:, fk:fk + NL], ["gl" + x] + ([] if k else seq("Y%d", range(P))))
         tt("gs" + x, row(T.tmp, k), T.V[:, 0:WN].indirect(c16), row(T.Ex, k), A.mult,
-           ["ex" + x] + (["ps" + before] if k else ["l_v1", "z_V"]))
+           ["ex" + x] + (["ps" + before] if k else ["l_v1", "z_Vs", "zL", "scn%d" % last, "u%d" % last]))
         tt("ps" + x, T.V[:, 0:WN].indirect(c16), row(T.tmp, k), row(T.W2, k), A.add,
            ["gs" + x, "W2" + x] + (nbV[k - 1] + nbS[k - 1] if k else []))
         ready = {p: [] for p in range(4)}
@@ -340,6 +351,12 @@ def rank_program(g, core, T, topo):
                 ready[p].append(name)
 
         for p0, p1, how in NBR[k]:
+            if p1 - p0 == 4:
+                name = "n" + x
+                act(name, ag(k, 0, 0, 16), T.V[:, 0:WN].indirect(T.nb[:, k, :]), ["ps" + x] + seq("nb%d" + batch[k], range(4)))
+                nbS[k].append(name)
+                ready = {p: [name] for p in range(4)}
+                continue
             for n in range(4):
                 neighbours(n, p0, p1, how)
         eng = engines(r, SENDS[k])
@@ -377,24 +394,29 @@ def rank_program(g, core, T, topo):
     def nbs(x):
         return seq("nb%d" + x, range(4))
 
+    def weave(*lists):
+        return [x[i] for i in range(max(len(x) for x in lists)) for x in lists if i < len(x)]
+
     order = {
-        "y": ["l_s0", "r_tL", "l_s1", "r_tH", "r_s0H", "r_s0L", "l_last", "l_rate", "l_v0", "r_s1H", "r_s1L", "cpW2", "cpW3",
-              "l_v1", "r_lH", "r_lL", "sts0", "sts1", "sts2", "stv3"],
-        "g": ["i_p", "i_cnt", "i_e", "i_blk", "i_k"] + seq("Sm%d", range(SM_G, 16)) + ["M1", "M2", "i_d0", "i_d1", "z_Lg"]
-        + ["sendE0", "i_d2", "sendE1", "z_V", "sendE2", "sendE3"] + [n for n in ops if n[:5] == "sendA"],
-        "t": ["y00", "y01", "sh0", "pc0", "pm0", "sh1", "y10", "y11", "y20", "pc1", "pm1", "sh2", "y21", "pc2", "pm2", "y30", "y31",
-              "pl0", "dA0", "w0", "pl1", "dL0", "w1", "dA1", "pl2", "dL1", "w2", "pl3", "dA2", "dL2", "w3", "dA3", "dL3"]
-        + [n for n in ops if n[:2] == "oa"],
-        "v": ["z_B", "oI", "pf", "of", "gf", "m16", "Bf", "eb", "mT", "mU", "s0H", "s0L", "NEG", "zp", "t128", "zI", "gn", "zH",
-              "gm", "zL", "gb", "t16"] + seq("Sm%d", range(SM_S, SM_G)) + ["s1H", "s1L", "pixr", "lastH", "lastL"]
-        + cls("0") + slots("0") + ["put0"] + cls("1") + slots("1") + cls("2") + ["put1"] + slots("2") + ["put2"] + dec("0")
-        + ["put3", "x1", "nb00", "c1", "nb10", "c161", "pL0", "nb20", "gs0", "nb30", "ps0"] + dec("2") + ["pL1"] + nbV[0]
-        + dec("3") + nbs("1") + ["gs1", "ps1", "pL2", "Id"] + nbV[1] + nbs("2") + ["gs2"] + nbs("3") + ["ps2"] + nbV[2]
-        + ["gs3", "ps3"] + nbV[3] + ["pickv3"],
-        "s": ["l_tm", "l_pol", "l_pix", "tH"] + seq("Sm%d", range(SM_S)) + ["Bm"] + seq("E0%d", range(4)) + ["G0", "G1"]
-        + seq("E1%d", range(4)) + ["Y0", "G2", "G3", "Y1", "z_Ls", "Y2", "Dsel", "Wsel", "Y3"]
-        + ["gl0", "W20", "ex0", "gl1", "W21", "ex1"] + nbS[0] + ["gl2", "W22", "ex2"] + nbS[1] + ["gl3", "W23", "ex3"]
-        + nbS[2] + ["oc0", "oc1", "picks0"] + nbS[3] + ["oc2", "picks1", "picks2", "oc3", "picks3", "sts3"],
+        "y": ["l_s0", "l_last", "r_tL", "l_s1", "r_tH", "r_s0H", "r_s0L", "l_v0"] + seq("cpW%d", range(1, P))
+        + ["r_s1H", "r_s1L", "l_v1", "r_lH", "r_lL", "l_rate", "sts0", "sts2", "stv1", "stv3"],
+        "g": ["i_p", "i_cnt", "i_e", "i_k", "i_blk"] + seq("Sm%d", range(SM_G, 16)) + ["M1", "M2", "i_d1", "z_Lg", "i_d2"]
+        + [n for n in ops if n[:4] == "send"],
+        "t": ["y00", "y01", "sh0", "sh1", "pc0", "pm0", "y10", "y11", "pc1", "pm1", "sh2", "y20", "y21", "pc2", "pm2", "y30", "y31",
+              "pl0", "w0", "pl1", "w1", "dA0", "dL0", "w2", "dA1", "dL1", "pl2", "pl3", "w3", "dA2", "dL2", "dA3", "dL3"]
+        + seq("oa%d", range(P)),
+        "v": ["oI", "pf", "of", "gf", "m16", "Bf", "z_B"]
+        + weave(["s0H", "s0L", "zp", "zI", "zH", "zL", "t16"], ["mT", "eb", "mU", "t128", "gn", "gb", "gm"])
+        + ["NEG", "s1H", "pixr", "lastH", "s1L", "lastL"] + cls("0") + weave(cls("1"), slots("0")) + ["put0"]
+        + weave(slots("1"), ["Id"] + cls("2")) + ["put1"] + slots("2") + ["put2"] + dec("0")
+        + ["put3", "x1", "nb00", "nb10", "c1", "pL0", "c161", "gs0", "nb20", "nb30", "ps0"]
+        + weave(dec("2"), nbs("1")[:2]) + ["pL1", "gs1"] + nbs("1")[2:] + ["ps1", "gs2", "pL2"] + nbs("2") + ["ps2"]
+        + nbV[2][:3] + ["gs3"] + nbV[2][3:] + ["ps3"] + weave(nbV[3][:3], nbV[3][6:]) + nbV[3][3:6] + ["pickv1", "pickv3"],
+        "s": ["l_tm", "l_pol", "l_pix", "tH"] + seq("Sm%d", range(SM_S)) + seq("E%d", range(4))
+        + ["Bm", "G0", "G1", "Wsel", "Dsel", "Y0", "G2", "G3", "Y1", "z_Vs", "Y2", "Y3"]
+        + ["W20", "gl0", "W21", "ex0", "gl1", "W22", "ex1", "n0", "gl2", "ex2", "n1", "gl3", "W23"]
+        + nbS[2][:1] + ["ex3"] + nbS[2][1:] + ["oc0", "picks0", "n320", "n310", "n330"] + nbS[3][3:]
+        + ["oc1", "oc2", "picks2", "oc3", "picks3", "sts3"],
     }
 
     token, total = {s: (s, n) for s, n in arrive.items()}, {}

from concourse.bass import DstId, RemoteDMATransfer
from concourse.mybir import AluOpType as A
from concourse.mybir import ActivationFunctionType as F

P, E, S, TT, CAP = 4, 512, 4096, 2048, 160
NL = 4 * CAP
WN = S + 3 * 256 + CAP
WK = 7 * CAP
AK = 3 * CAP + 4 * NL
BIG = 1025.0
T_HI, T_LO, PIX_HI, PIX_LO = 2, 6, 7, 9
SW = 134
BF = "bfloat16"

SRC = [[0], [1], [2, 3]]
DEC = [[0], [1], [2, 3]]
SM_S, SM_G = 9, 9
NBR = [[(0, 4, "s")], [(0, 4, "s")], [(2, 4, "v"), (0, 2, "s")], [(2, 3, "h"), (3, 4, "h"), (1, 2, "h"), (0, 1, "s")]]
SENDS = [[[1, 2, 3]]] * 3 + [[[2], [3, 1]]]
EV_MOST = [4, 4, 8, 8]
PICK = [[("s", 0, 32)], [("v", 0, 32)], [("s", 0, 32)]] + [[("v", 0, 16), ("s", 16, 32)]]


def _sb(cols, dt="float32"):
    return ("sbuf", [128] + (list(cols) if isinstance(cols, (list, tuple)) else [cols]), dt)


SCRATCH = {
    "tmI": _sb(128, "int32"), "pixI": _sb(128, "int32"), "polI": _sb(128, "int32"),
    "lastI": _sb(256, "int32"), "ratec": _sb(4), "s0I": _sb(256, "int32"), "s1I": _sb(256, "int32"),
    "lastH": _sb(256, BF), "lastL": _sb(256, BF),
    "zH": _sb(128, BF), "zL": _sb(128, BF), "t16": _sb(128, "uint16"),
    "pI": _sb(4, "int32"), "oI": _sb(4, "int32"), "col": _sb(8), "m16": _sb(16), "gm": _sb(4), "gn": _sb(4),
    "gb": _sb(4), "eb": _sb(4), "io8": _sb(8), "cnt": _sb(CAP, BF),
    "Bm": _sb(144, BF), "NEG": _sb(128, BF), "M2": _sb(128, BF),
    "Dsel": _sb(128, BF), "Wsel": _sb(128, BF), "Sm": _sb(9 * SW, BF),
    "G": _sb(P * E, BF), "Y": _sb(P * E, BF), "Id": _sb(128), "W": _sb(P * WK, BF),
    "uI": _sb(128, "int32"), "qI": _sb(128, "int32"), "slot": _sb(128, "uint16"),
    "xI": _sb([P, 40], "int32"), "cI": _sb([P, 40], "int32"), "c16": _sb([P, 40], "uint16"), "nb": _sb([P, 160], "uint16"),
    "V": _sb(WN), "L": _sb(S + 7 * SW, BF), "Lg": _sb(P * NL, BF), "Ex": _sb(P * NL), "W2": _sb(P * NL), "tmp": _sb(P * NL),
    "yst": _sb(P * E),
    "PA": ("psum", [128, 1024], "float32"), "PB": ("psum", [128, 1024], "float32"),
}
for _k in range(P):
    SCRATCH["an%d" % _k] = _sb(AK)
for _b, _ks in enumerate(SRC):
    _n = 32 * len(_ks)
    SCRATCH.update({"ind%d" % _b: _sb(4 * _n, BF), "scn%d" % _b: _sb(4 * _n),
                    "pos%d" % _b: _sb(4 * _n), "ma%d" % _b: _sb(2 * _n), "mb%d" % _b: _sb(_n)})
for _x in ("PS0", "PS1", "PC", "PM"):
    SCRATCH[_x] = ("psum", [128, 512], "float32")
SEMAPHORES = ["cv", "cs", "ct", "cg", "ltm", "ls0", "ls1", "lpix", "lpol", "llast", "lv", "lrate", "rowB", "rowC", "rowL", "cpW",
              "sent", "st"] + ["%s%d" % (_x, _k) for _x in ("ev", "an") for _k in range(P)]


def seq(pat, xs):
    return [pat % x for x in xs]


def _bits(es):
    m = 0
    for e in es:
        m |= 1 << e
    return m


def _share(topo, src, dsts, most):
    far = [d for d in dsts if topo.chip(d) != topo.chip(src)]
    near = [d for d in dsts if topo.chip(d) == topo.chip(src)]
    out, used = {}, []
    for grp in (far, near):
        for i, d in enumerate(grp):
            free = [e for e in topo.engines(src, d) if e not in used]
            n = min(len(free) // (len(grp) - i), most)
            while n & (n - 1):
                n -= 1
            out[d] = free[:n]
            used += free[:n]
    return out


def rank_program(g, core, T, topo):
    r = T.rank_of(core)
    if r is None:
        return
    cores = list(T.cores)
    N = len(cores)
    Q = {"v": g.vector, "s": g.scalar, "t": g.tensor, "g": g, "y": g.sync}
    V, SC, PE = g.vector, g.scalar, g.tensor
    ops = {}

    def op(name, q, fn, dep=(), sem=None):
        ops[name] = (q, fn, list(dep), sem)

    def ts(name, out, in0, s1, s2, op0, op1=None, dep=()):
        if op1 is None:
            op(name, "v", lambda: V.tensor_scalar(out, in0, s1, None, op0), dep)
        else:
            op(name, "v", lambda: V.tensor_scalar(out, in0, s1, s2, op0, op1), dep)

    def tt(name, out, in0, in1, o, dep=()):
        op(name, "v", lambda: V.tensor_tensor(out, in0, in1, o), dep)

    def cp(name, out, in_, dep=()):
        op(name, "v", lambda: V.tensor_copy(out, in_), dep)

    def act(name, out, in_, dep=(), func=F.Identity, **kw):
        op(name, "s", lambda: SC.activation(out, in_, func, **kw), dep)

    def iota(name, out, pat, base=0, cm=0):
        op(name, "g", lambda: g.iota(out, pat, base, cm, allow_small_or_imprecise_dtypes=True))

    def dma(name, q, out, in_, sem, dep=(), **kw):
        op(name, q, lambda: Q[q].dma_start(out, in_, **kw), dep, sem)

    def mm(name, items, dep):
        def fn():
            for out, lhsT, rhs, start, stop in items:
                ins = PE.matmul(out, lhsT, rhs, start, stop)
            return ins
        op(name, "t", fn, dep)

    def to_lists(name, out, buf, c0, n, dep):
        mm(name, [(out, T.Bm[:, 15 - o:143 - o], buf[:, c0 + o:c0 + n:16], o == 0, o == 15) for o in range(16)], dep + ["Bm"])

    sent = [0]

    def remote(name, items, sem, dep):
        trs = []
        for d, es, srcs, dst in items:
            rid, pid, _ = topo.addr(d)
            trs.append(RemoteDMATransfer(dst_ids=[DstId(rid=rid, pnc=pid)], dma_engine_mask=_bits(es),
                                         remote_sem=T.sem[sem], srcs=srcs, dsts=[dst], alu_op=1 if len(srcs) > 1 else 0))
            sent[0] += len(es)
        op(name, "g", lambda: g.remote_dma_fused(trs, local_sem=T.sem.sent), dep, "remote")

    def senders(a):
        rest = [b for b in range(N) if b != a]
        return [a] + sorted(rest, key=lambda b: topo.chip(cores[b]) != topo.chip(cores[a]))

    def bucket(src, a):
        return 3 - (a - src) % N

    def engines(a, calls, most=8):
        out = {}
        for ps in calls:
            out.update(_share(topo, cores[a], [cores[senders(a)[p]] for p in ps], most))
        return out

    others = senders(r)[1:]
    arrive = {}
    for k in range(P):
        arrive["ev%d" % k] = sum(len(engines(a, [[1, 2, 3]], EV_MOST[k])[core]) for a in others)
        arrive["an%d" % k] = sum(len(engines(a, SENDS[k])[core]) for a in others)

    dma("l_s0", "y", T.s0I[:], T.sh[:, 0:2 * TT], "ls0")
    dma("l_s1", "y", T.s1I[:], T.sh[:, 2 * TT:4 * TT], "ls1")
    dma("l_tm", "s", T.tmI[:], T.tm[:], "ltm")
    dma("l_pix", "s", T.pixI[:], T.pix[:], "lpix")
    dma("l_pol", "s", T.polI[:], T.pol[:], "lpol")
    dma("l_last", "y", T.lastI[:], T.last[:], "llast")
    for h in range(2):
        dma("l_v%d" % h, "y", T.V[:, S // 2 * h:S // 2 * (h + 1)], T.v[:, S // 2 * h:S // 2 * (h + 1)], "lv")
    dma("l_rate", "y", T.ratec[:, 0:1], T.rate[:], "lrate")

    def carve(buf, c0, **sizes):
        out = {}
        for name, n in sizes.items():
            out[name] = buf[:, c0:c0 + n]
            out[name + "0"] = c0
            c0 += n
        return out, c0

    U, end = carve(T.L, TT, s0H=256, s0L=256, s1H=256, s1L=256, tH=128, blk=128, M1=128, Bf=144)
    U.update(carve(T.V, S + CAP, d1=128, d2=256, pixr=128, zp=128, zI=128)[0])

    def Sm(j, c0=0, n=SW):
        buf, c = (T.L, S + SW * j) if j < 7 else (T.Sm, SW * (j - 7))
        return buf[:, c + c0:c + c0 + n]

    pf, of, gf, mT, mU, t128 = (T.col[:, i:i + 1] for i in range(6))
    op("i_p", "g", lambda: g.iota(T.pI[:, 0:1], [[0, 1]], 0, 1))
    iota("i_cnt", T.cnt[:], [[1, CAP]])
    iota("i_blk", U["blk"], [[16, 8], [0, 16]])
    iota("i_k", T.io8[:, 0:4], [[TT, 4]])
    iota("i_e", T.io8[:, 4:8], [[256 - S, 4]], S * (r + 4))
    for n in (1, 2):
        iota("i_d%d" % n, U["d%d" % n], [[-CAP, 4], [0, n], [1000, 32]], 3 * CAP)
    iota("z_Lg", T.L[:, end:S], [[0, S - end]])
    op("z_B", "v", lambda: V.memset(T.L[:, 0:TT], 0.0))
    act("z_Vs", T.V[:, S:S + CAP], T.cnt[:], ["i_cnt"], F.Exp, scale=0.0)
    ts("oI", T.oI[:, 0:1], T.pI[:, 0:1], 15, None, A.bitwise_and, dep=["i_p"])
    cp("pf", pf, T.pI[:, 0:1], ["i_p"])
    cp("of", of, T.oI[:, 0:1], ["oI"])
    tt("gf", gf, pf, of, A.subtract, ["pf", "of"])
    ts("m16", T.m16[:], T.cnt[:, 0:16], of, None, A.is_equal, dep=["of", "i_cnt"])

    def m(o):
        return T.m16[:, o:o + 1]

    ts("Bf", U["Bf"], T.cnt[:, 0:144], -15.0, gf, A.add, A.is_equal, dep=["gf", "i_cnt"])
    ts("eb", T.eb[:], T.io8[:, 4:8], m(PIX_HI), None, A.mult, dep=["m16", "i_e"])
    tt("mT", mT, m(T_HI), m(T_LO), A.add, ["m16"])
    ts("mU", mU, mT, 0.0, None, A.is_equal, dep=["mT"])
    ts("t128", t128, m(T_HI), 127.0, mT, A.mult, A.add, dep=["mT"])
    tt("gn", T.gn[:], T.m16[:, 0:16:4], T.m16[:, 1:16:4], A.add, ["m16"])
    ts("gm", T.gm[:], T.gn[:], t128, None, A.add, dep=["gn", "t128"])
    ts("gb", T.gb[:], T.io8[:, 0:4], m(T_HI), None, A.mult, dep=["m16", "i_k"])
    ts("NEG", T.NEG[:], U["blk"], gf, -1.0, A.is_equal, A.mult, dep=["gf", "i_blk"])
    ts("Id", T.Id[:], T.cnt[:, 0:128], pf, None, A.is_equal, dep=["pf", "i_cnt"])
    op("M1", "g", lambda: g.affine_select(U["M1"], T.NEG[:], [[-1, 128]], A.is_gt, 0.0, 0, 1), ["NEG"])
    op("M2", "g", lambda: g.affine_select(T.M2[:], U["M1"], [[-1, 128]], A.not_equal, BIG - 1.0, 0, 1), ["M1"])
    act("tH", U["tH"], T.cnt[:, 0:128], ["of", "i_cnt"], scale=0.0, bias=of)
    act("Bm", T.Bm[:], U["Bf"], ["Bf", "mU"], scale=mU)
    act("Dsel", T.Dsel[:], T.NEG[:], ["NEG", "mT"], scale=mT)
    act("Wsel", T.Wsel[:], T.NEG[:], ["NEG", "m16"], scale=m(PIX_HI))
    src = T.L[:, U["Bf0"] + 15 - PIX_LO:U["Bf0"] + 15 - PIX_LO + SW]
    for j in range(16):
        if j >= SM_G:
            op("Sm%d" % j, "g", lambda j=j, src=src: g.affine_select(Sm(j), src, [[1, SW]], A.is_equal, 0.0, j - PIX_LO, -1),
               ["Bf"])
        elif j < SM_S:
            act("Sm%d" % j, Sm(j), src, ["Bf", "m16"], scale=m(j))
        else:
            ts("Sm%d" % j, Sm(j), src, m(j), None, A.mult, dep=["Bf", "m16"])
    for j in range(4):
        act("E%d" % j, T.W[:, CAP * j:CAP * (j + 1)], T.cnt[:], ["eb", "i_cnt"], scale=m(PIX_LO), bias=T.eb[:, j:j + 1])
    for k in range(1, P):
        dma("cpW%d" % k, "y", T.W[:, WK * k:WK * k + NL], T.W[:, 0:NL], "cpW", seq("E%d", range(4)))

    ts("zp", U["zp"], T.polI[:], 16384.0, -16384.0, A.mult, A.add, dep=["l_pol"])
    tt("zI", U["zI"], T.pixI[:], U["zp"], A.add, ["zp", "l_pix"])
    for x, ld in (("s0", "l_s0"), ("s1", "l_s1"), ("last", "l_last"), ("z", "zI")):
        whole, hi, lo = (U[x + y] if x + y in U else T[x + y][:] for y in "IHL")
        cp(x + "H", hi, whole, [ld])
        tt(x + "L", lo, whole, hi, A.subtract, [x + "H"])
    cp("t16", T.t16[:], T.tmI[:], ["l_tm"])
    ts("pixr", U["pixr"], T.pixI[:], float(S * ((N - r) % N)), None, A.add, dep=["l_pix"])
    dma("r_tH", "y", T.L[T_HI::16, 0:TT], U["tH"], "rowB", ["z_B", "tH"])
    dma("r_tL", "y", T.L[T_LO::16, 0:TT], T.cnt[:, 0:128], "rowB", ["z_B", "i_cnt"])
    dma("r_s0H", "y", T.L[0::8, 0:TT], U["s0H"], "rowB", ["z_B", "s0H"])
    dma("r_s0L", "y", T.L[1::8, 0:TT], U["s0L"], "rowB", ["z_B", "s0L"])
    dma("r_s1H", "y", T.L[4::8, 0:TT], U["s1H"], "rowC", ["G0", "G1", "s1H"])
    dma("r_s1L", "y", T.L[5::8, 0:TT], U["s1L"], "rowC", ["G0", "G1", "s1L"])
    done = ["z_Lg", "M2", "Bm"] + seq("G%d", range(P)) + seq("Sm%d", range(16))
    dma("r_lH", "y", T.L[T_HI::16, 0:S], T.lastH[:], "rowL", done + ["lastH"])
    dma("r_lL", "y", T.L[T_LO::16, 0:S], T.lastL[:], "rowL", done + ["lastL"])

    PY = [T.PA, T.PB]
    PS = [T.PS0, T.PS1]
    for k in range(P):
        es, ls, c0 = slice(E * k, E * (k + 1)), slice(32 * k, 32 * k + 32), E * (k % 2)
        act("G%d" % k, T.G[:, es], T.L[:, 0:TT].indirect(T.t16[:, ls]), ["r_s%dL" % (k // 2), "t16", "gm", "gb"],
            scale=T.gm[:, 2 * (k % 2) + k // 2:2 * (k % 2) + k // 2 + 1], bias=T.gb[:, k:k + 1])
        for h in range(2):
            js = range(8 * h, 8 * h + 8)
            mm("y%d%d" % (k, h), [(PY[k // 2][:, c0 + j:c0 + E:16], Sm(j, PIX_LO - to, 128), T[f][:, ls], i == 0, i == 1)
                                  for j in js for i, (f, to) in enumerate((("zH", PIX_HI), ("zL", PIX_LO)))],
               seq("Sm%d", js) + ["zH", "zL"])
        act("Y%d" % k, T.Y[:, es], PY[k // 2][:, c0:c0 + E], seq("y%d%%d" % k, range(2)))
    counted = {}
    for b, ks in enumerate(SRC):
        n, x = 32 * len(ks), str(b)
        ls = slice(32 * ks[0], 32 * ks[0] + n)
        ind, scn, pos, ma, mb = (T[y + x] for y in ("ind", "scn", "pos", "ma", "mb"))
        to_lists("sh" + x, PS[b % 2][:, 0:n], T.G, E * ks[0], 16 * n, seq("G%d", ks) + (["u%d" % (b - 2)] if b > 1 else []))
        tt("u" + x, T.uI[:, ls], PS[b % 2][:, 0:n], T.V[:, U["pixr0"] + ls.start:U["pixr0"] + ls.stop], A.add, ["sh" + x, "pixr"])
        ts("q" + x, T.qI[:, ls], T.uI[:, ls], 12, 3, A.arith_shift_right, A.bitwise_and, dep=["u" + x])
        for i in range(4):
            ts("ind%d" % i + x, ind[:, n * i:n * (i + 1)], T.qI[:, ls], float(i), None, A.is_equal, dep=["q" + x])
        inds = seq("ind%d" + x, range(4))
        mm("pc" + x, [(T.PC[:, 0:4 * n], T.NEG[:], ind[:], True, True)], inds + ["NEG"] + (["scn%d" % (b - 1)] if b else []))
        mm("pm" + x, [(T.PM[:, 0:4 * n], T.M2[:], ind[:], True, True)], inds + ["M2"] + (["pos%d" % (b - 1)] if b else []))
        op("scn" + x, "v", lambda scn=scn, n=n: V.tensor_tensor_scan(scn[:], U["d%d" % (n // 32)], T.PC[:, 0:4 * n], 1.0e4,
                                                                    A.min, A.subtract), ["pc" + x, "i_d%d" % len(ks)])
        tt("pos" + x, pos[:], scn[:], T.PM[:, 0:4 * n], A.add, ["scn" + x, "pm" + x])
        tt("ma" + x, ma[:], pos[:, 0:2 * n], pos[:, 2 * n:4 * n], A.max, ["pos" + x])
        tt("mb" + x, mb[:], ma[:, 0:n], ma[:, n:2 * n], A.max, ["ma" + x])
        ts("slot" + x, T.slot[:, ls], mb[:], -BIG, None, A.add, dep=["mb" + x])
        for k in ks:
            counted[k] = "slot" + x
            tt("put%d" % k, T.W[:, WK * k:WK * k + NL].indirect(T.slot[:, 32 * k:32 * k + 32]), T.G[:, E * k:E * (k + 1)],
               T.Y[:, E * k:E * (k + 1)], A.add, ["slot" + x, "G%d" % k, "Y%d" % k, "cpW3"])

    def ev(k, c0, n=CAP):
        return T.W[:, WK * k + c0:WK * k + c0 + n]

    for k in range(P):
        eng = engines(r, [[1, 2, 3]], EV_MOST[k])
        remote("sendE%d" % k, [(cores[a], eng[cores[a]], [ev(k, CAP * bucket(r, a))],
                               ev(k, CAP * (3 + senders(a).index(r)))) for a in others], "ev%d" % k, ["put%d" % k])

    def row(buf, k):
        return buf[:, NL * k:NL * (k + 1)]

    last = len(SRC) - 1
    readers = ["u%d" % (last - last % 2), "u%d" % (last - (last + 1) % 2)]
    batch = {}
    for b, ks in enumerate(DEC):
        x, kk, bank = str(b), slice(ks[0], ks[-1] + 1), PS[b % 2]
        for i, k in enumerate(ks):
            batch[k] = x
            to_lists("pl%d" % k, bank[:, 40 * i:40 * i + 40], T.W, WK * k + 3 * CAP, NL,
                     ["ev%d" % k, "put%d" % k, readers[b % 2]])
        ts("x" + x, T.xI[:, kk, :], bank[:, 0:40 * len(ks)], -float(S * r), None, A.add, dep=seq("pl%d", ks))
        readers[b % 2] = "x" + x
        ts("c" + x, T.cI[:, kk, :], T.xI[:, kk, :], 4 * S - 1, None, A.bitwise_and, dep=["x" + x])
        cp("c16" + x, T.c16[:, kk, :], T.cI[:, kk, :], ["c" + x])
        for n, (d, lim, o) in enumerate(((-1.0, 0, A.max), (1.0, S - 1, A.min), (-128.0, 0, A.max), (128.0, S - 1, A.min))):
            ts("nb%d" % n + x, T.nb[:, kk, 40 * n:40 * n + 40], T.cI[:, kk, :], d, float(lim), A.add, o, dep=["c" + x])

    def ag(k, n, p0, p1=None):
        c0 = 3 * CAP + NL * n
        return T["an%d" % k][:, c0 + CAP * p0:c0 + CAP * (p0 + 1 if p1 is None else p1)]

    halves = ((0, 512), (512, NL))
    used = ["scn%d" % last, "pos%d" % last]
    nbV, nbS = [[] for _ in range(P)], [[] for _ in range(P)]
    for k in range(P):
        x, c16, before = str(k), T.c16[:, k, :], str(k - 1)
        fk, here = WK * k + 3 * CAP, ["ev" + x, "put" + x]
        mm("dA" + x, [(T.PA[:, a:b], T.Dsel[:], T.W[:, fk + a:fk + b], True, False) for a, b in halves],
           here + ["Dsel"] + (["ex" + before] if k else ["Y0", "Y1"]))
        mm("w" + x, [(T.PB[:, a:b], T.Wsel[:], T.W[:, fk + a:fk + b], True, True) for a, b in halves],
           here + ["Wsel"] + (["W2" + before] if k else ["Y2", "Y3"]))
        act("W2" + x, row(T.W2, k), T.PB[:, 0:NL], ["w" + x], F.Sign, scale=-1.0, bias=0.5)
        act("gl" + x, row(T.Lg, k), T.L[:, 0:WN].indirect(c16), ["c16" + batch[k], "pL" + before if k else "r_lL"], scale=-1.0)
        mm("dL" + x, [(T.PA[:, a:b], T.Dsel[:], T.Lg[:, NL * k + a:NL * k + b], False, True) for a, b in halves],
           ["gl" + x, "dA" + x])
        act("ex" + x, row(T.Ex, k), T.PA[:, 0:NL], ["dL" + x, "l_rate"], F.Exp, scale=T.ratec[:, 0:1])
        if k < P - 1:
            cp("pL" + x, T.L[:, 0:WN].indirect(c16), T.W[:, fk:fk + NL], ["gl" + x] + ([] if k else seq("Y%d", range(P))))
        tt("gs" + x, row(T.tmp, k), T.V[:, 0:WN].indirect(c16), row(T.Ex, k), A.mult,
           ["ex" + x] + (["ps" + before] if k else ["l_v1", "z_Vs", "zL", "scn%d" % last, "u%d" % last]))
        tt("ps" + x, T.V[:, 0:WN].indirect(c16), row(T.tmp, k), row(T.W2, k), A.add,
           ["gs" + x, "W2" + x] + (nbV[k - 1] + nbS[k - 1] if k else []))
        ready = {p: [] for p in range(4)}
        fused = [p for p0, p1, how in NBR[k] if how != "s" for p in range(p0, p1)]

        def neighbours(n, p0, p1, how):
            name, dep = "n%d%d%d" % (k, p0, n), ["ps" + x, "nb%d" % n + batch[k]]
            src = T.V[:, 0:WN].indirect(T.nb[:, k, 40 * n + 10 * p0:40 * n + 10 * p1])
            if how == "s" or (how, n) == ("h", 0):
                act(name, ag(k, n, p0, p1), src, dep)
            elif n == 0:
                cp(name, ag(k, 0, p0, p1), src, dep)
            else:
                tt(name, ag(k, 0, p0, p1), src, ag(k, 0, p0, p1), A.add, dep + ["n%d%d%d" % (k, p0, n - 1)])
            (nbV if ops[name][0] == "v" else nbS)[k].append(name)
            for p in range(p0, p1):
                ready[p].append(name)

        for p0, p1, how in NBR[k]:
            if p1 - p0 == 4:
                name = "n" + x
                act(name, ag(k, 0, 0, 16), T.V[:, 0:WN].indirect(T.nb[:, k, :]), ["ps" + x] + seq("nb%d" + batch[k], range(4)))
                nbS[k].append(name)
                ready = {p: [name] for p in range(4)}
                continue
            for n in range(4):
                neighbours(n, p0, p1, how)
        eng = engines(r, SENDS[k])
        for i, ps in enumerate(SENDS[k]):
            items = []
            for p in ps:
                a = senders(r)[p]
                items.append((cores[a], eng[cores[a]], [ag(k, n, p) for n in range(1 if p in fused else 4)],
                              T["an" + x][:, CAP * bucket(a, r):CAP * (bucket(a, r) + 1)]))
            remote("sendA%d%d" % (k, i), items, "an" + x, [d for p in ps for d in ready[p]])
        own = ready[0]
        if 0 not in fused:
            bank = [T.PC, T.PM][k % 2]
            mm("oa" + x, [(bank[:, 0:CAP], T.Id[:], ag(k, n, 0), n == 0, n == 3) for n in range(4)],
               own + ["Id", used[k % 2]])
            act("oc" + x, ag(k, 0, 0), bank[:, 0:CAP], ["oa" + x])
            own = ["oc" + x]
            used[k % 2] = "oc" + x
        for q, c0, c1 in PICK[k]:
            out = T.yst[:, E * k + 16 * c0:E * k + 16 * c1]
            src = T["an" + x][:, 0:NL].indirect(T.slot[:, 32 * k + c0:32 * k + c1])
            (cp if q == "v" else act)("pick" + q + x, out, src, ["an" + x, counted[k]] + own)
            dma("st" + q + x, "s" if (q, k) == ("s", P - 1) else "y", T.y[:, E * k + 16 * c0:E * k + 16 * c1], out, "st",
                ["pick" + q + x])

    def cls(x):
        return ["u" + x, "q" + x] + seq("ind%d" + x, range(4))

    def slots(x):
        return [y + x for y in ("scn", "pos", "ma", "mb", "slot")]

    def dec(x):
        return ["x" + x, "c" + x, "c16" + x]

    def nbs(x):
        return seq("nb%d" + x, range(4))

    def weave(*lists):
        return [x[i] for i in range(max(len(x) for x in lists)) for x in lists if i < len(x)]

    order = {
        "y": ["l_s0", "l_last", "r_tL", "l_s1", "r_tH", "r_s0H", "r_s0L", "l_v0"] + seq("cpW%d", range(1, P))
        + ["r_s1H", "r_s1L", "l_v1", "r_lH", "r_lL", "l_rate", "sts0", "sts2", "stv1", "stv3"],
        "g": ["i_p", "i_cnt", "i_e", "i_k", "i_blk"] + seq("Sm%d", range(SM_G, 16)) + ["M1", "M2", "i_d1", "z_Lg", "i_d2"]
        + [n for n in ops if n[:4] == "send"],
        "t": ["y00", "y01", "sh0", "sh1", "pc0", "pm0", "y10", "y11", "pc1", "pm1", "sh2", "y20", "y21", "pc2", "pm2", "y30", "y31",
              "pl0", "w0", "pl1", "w1", "dA0", "dL0", "w2", "dA1", "dL1", "pl2", "pl3", "w3", "dA2", "dL2", "dA3", "dL3"]
        + seq("oa%d", range(P)),
        "v": ["oI", "pf", "of", "gf", "m16", "Bf", "z_B"]
        + weave(["s0H", "s0L", "zp", "zI", "zH", "zL", "t16"], ["mT", "eb", "mU", "t128", "gn", "gb", "gm"])
        + ["NEG", "s1H", "pixr", "lastH", "s1L", "lastL"] + cls("0") + weave(cls("1"), slots("0")) + ["put0"]
        + weave(slots("1"), ["Id"] + cls("2")) + ["put1"] + slots("2") + ["put2"] + dec("0")
        + ["put3", "x1", "nb00", "nb10", "c1", "pL0", "c161", "gs0", "nb20", "nb30", "ps0"]
        + weave(dec("2"), nbs("1")[:2]) + ["pL1", "gs1"] + nbs("1")[2:] + ["ps1", "gs2", "pL2"] + nbs("2") + ["ps2"]
        + nbV[2][:3] + ["gs3"] + nbV[2][3:] + ["ps3"] + weave(nbV[3][:3], nbV[3][6:]) + nbV[3][3:6] + ["pickv1", "pickv3"],
        "s": ["l_tm", "l_pol", "l_pix", "tH"] + seq("Sm%d", range(SM_S)) + seq("E%d", range(4))
        + ["Bm", "G0", "G1", "Wsel", "Dsel", "Y0", "G2", "G3", "Y1", "z_Vs", "Y2", "Y3"]
        + ["W20", "gl0", "W21", "ex0", "gl1", "W22", "ex1", "n0", "gl2", "ex2", "n1", "gl3", "W23"]
        + nbS[2][:1] + ["ex3"] + nbS[2][1:] + ["oc0", "picks0", "n320", "n310", "n330"] + nbS[3][3:]
        + ["oc1", "oc2", "picks2", "oc3", "picks3", "sts3"],
    }

    token, total = {s: (s, n) for s, n in arrive.items()}, {}
    for q, names in order.items():
        for name in names:
            sem = ops[name][3] or "c" + q
            total[sem] = total.get(sem, 0) + (16 if ops[name][3] else 1)
            token[name] = (sem, total[sem])
    for name, (q, fn, dep, sem) in ops.items():
        if sem:
            token[name] = (sem, total[sem])
    top = {}
    for q, names in order.items():
        seen = {}
        for name in names:
            _, fn, dep, sem = ops[name]
            for s, n in sorted((token[d] for d in dep), reverse=True):
                if (q, s) != ("t", "ct") and seen.get(s, 0) < n:
                    Q[q].wait_ge(T.sem[s], n)
                    seen[s] = n
                    top[s] = max(top.get(s, 0), n)
            ins = fn()
            if sem != "remote":
                ins.then_inc(T.sem[sem or "c" + q], 16 if sem else 1)
    total["sent"] = sent[0]
    for s, n in total.items():
        if s != "remote" and top.get(s, 0) < n:
            g.wait_ge(T.sem[s], n)
